import numpy as np, ml_dtypes
CORES = [242,247,114,119]
N = 4
import mx_ref
BF = ml_dtypes.bfloat16
def entries(a):
    return np.ascontiguousarray(a.T).reshape(-1)
def table(e):
    return np.ascontiguousarray(np.reshape(e, (-1, 16)).T).astype(np.int32)
def cols(t, e):
    v = np.concatenate([t.reshape(128, -1, 4), np.zeros((128, 1, 4), BF)], axis=1)
    return np.ascontiguousarray(v[:, e]).reshape(128, -1)
def cut(t, i, w=512):
    return t[:, w * i:w * i + w]
def f(rng, *shape):
    return mx_ref.flush((rng.standard_normal(shape, dtype=np.float32) * np.exp2(rng.integers(-2, 3, shape[:-1] + (1,)))).astype(BF))
def wide(rng, *shape, cols=0):
    v = rng.standard_normal(shape, dtype=np.float32) * np.exp2(rng.integers(-12, 13, shape)).astype(np.float32)
    if cols: v *= np.repeat(np.exp2(rng.integers(-cols, cols + 1, shape[:-2] + (1, shape[-1] // 4))) * (rng.random(shape[:-2] + (1, shape[-1] // 4)) > 0.0625), 4, axis=-1).astype(np.float32)
    return mx_ref.flush(v.astype(BF))
T, O = 256, 2
def places(rng, dest):
    e = np.zeros((N, T), int)
    for d in range(N): e[dest == d] = d * T + rng.permutation(T)
    return np.stack([table(e[r]) for r in range(N)])
def relabel(rng):
    p = rng.permutation(N)
    if np.all((p - np.arange(N)) % N == p[0]): p[[0, 1]] = p[[1, 0]]
    return p
def setup_inputs(rng):
    e = rng.permutation(N * T).reshape(N, T)
    return {"x": f(rng, N, 128, 4 * T), "to": np.stack([table(e[r]) for r in range(N)]), "w": f(rng, N, 128, 512 * O)}
def setup_inputs_swap(rng):
    d = setup_inputs(rng); p = rng.permutation(N); dest = np.zeros((N, T), int)
    for k in range(N): dest[p[k]] = p[(k + 1) % N]
    d["to"] = places(rng, dest); return d
def setup_inputs_ones(rng):
    d = setup_inputs(rng); i = np.arange(N); n = np.ones((N, N), int); n[i, rng.permutation(N)] += T % N
    for t in range(T // N - 1): n[i, rng.permutation(N)] += N
    d["to"] = places(rng, np.stack([rng.permutation(np.repeat(i, n[r])) for r in range(N)])); return d
def setup_inputs_runs(rng):
    d = setup_inputs(rng); p = relabel(rng); s, u = rng.integers(1, N), rng.integers(0, N); g, h = rng.permutation(N), rng.permutation(N)
    n = T // N + ((g[:, None] + h) % N < T % N)
    j = (np.arange(N) + s * np.arange(N)[:, None] + u) % N
    d["to"] = places(rng, np.stack([np.repeat(p[j[r]], n[r, j[r]]) for r in range(N)])); return d
def setup_inputs_comb(rng):
    d = setup_inputs(rng); p = relabel(rng); s, u = rng.integers(1, N), rng.integers(0, N); k = rng.permutation(N); c = np.arange(T)
    d["to"] = places(rng, np.stack([p[(c + np.where(c < T - T % N, s * r + u, k[r])) % N] for r in range(N)])); return d
def setup_inputs_spread(rng):
    d = setup_inputs(rng); d["x"] = wide(rng, N, 128, 4 * T, cols=8); return d
def check_inputs(d):
    e = np.concatenate([entries(d["to"][r]) for r in range(N)])
    return [] if np.array_equal(np.sort(e), np.arange(N * T)) else ["to"]
def reference(x, to, w):
    z = np.concatenate([x[r] for r in range(N)], axis=1)
    e = np.concatenate([entries(to[r]) for r in range(N)])
    home = np.zeros(N * T, int); home[e] = np.arange(N * T)
    y = np.zeros((N, 128, O * T), np.float32)
    for d in range(N):
        v = mx_ref.quantize(cols(z, home[d * T:d * T + T]))
        for o in range(O): y[d][:, T * o:T * o + T] = mx_ref.matmul(mx_ref.quantize(np.ascontiguousarray(cut(w[d], o))), v)
    return {"y": y}

@@ -1,0 +1,344 @@
+from concourse.bass import DstId, RemoteDMATransfer
+from concourse.mybir import dt, AluOpType, ActivationFunctionType
+
+N, COLS, O = 4, 256, 2
+PK1 = COLS // N
+PK2 = COLS // N + N - 1
+ST = 80
+LC = ST // 16
+NONE = -8192.0
+
+BUFFERS = {
+    "float8_e4m3fn_x4": "xq 256 wq 256 slot1q 256 land1q 256 slot2q 240 land2q 320 finq 256",
+    "uint8": "xs 256 ws 256 slot1s 256 land1s 256 slot2s 240 land2s 320 fins 256",
+    "bfloat16": "xb 1024 wb 1024 restart 128 ones 128 val2 256 ind 128 indt 128 ind2 128 cr 128 crt 128 cum 128 z 128 pp 128 "
+                "pm 128 pm2 64 pm3 32 win2 2048 wt2 2048 vout 64 vland 64 cn 4 cland 32",
+    "float32": "odd 1 even 1 odd8 1 odd16 1 lowf 1 tti 20 tt 20 pos 16 t1 16 t2 16 t3 16 t4 16 win1 512 wt1 512 l1f 16 ts 16 "
+               "o1 16 o2 16 cz 4 eb 21 nn 20 sf 20 xx 25 dd 20 h1 84 h2 42 h3 21 s4 20 cf 20 f1 64 f2 32 f3 16 yb 512 zero 512",
+    "int32": "part 1 par 1 low 1 val1 256 ew 32 ec 32 si 16 ui 16 hi 16 cb 30 aa 20 pb 30 vi 64 m3 64 m80 64 kk 64 ks 64",
+    "uint16": "off1 16 l1u 16 off2 16 l2u 22 flu 16",
+}
+SCRATCH = {"ps": ("psum", [128, 2048], "float32")}
+for _t, _l in BUFFERS.items():
+    _w = _l.split()
+    for _n, _c in zip(_w[0::2], _w[1::2]):
+        SCRATCH[_n] = ("sbuf", [128, int(_c)], _t)
+SEMAPHORES = "sv sa sg st ld_e ld_x ld_r ld_w cnt p1c p1s plc p2c p2s sent yo0 yo1".split()
+
+
+def plan(src, cores, topo):
+    near = set(topo.cores_of(src))
+    far = [d for d in cores if d not in near]
+    close = [d for d in cores if d in near and d != src]
+    out, used = {}, set()
+    for group in (far, close):
+        if group:
+            eng = [e for e in topo.engines(src, group[0]) if e not in used]
+            per = len(eng) // len(group)
+            for i, d in enumerate(group):
+                out[d] = eng[per * i:per * (i + 1)]
+            used.update(eng)
+    return out
+
+
+def rank_program(g, core, T, topo):
+    me = T.rank_of(core)
+    if me is None:
+        return
+    A, F = AluOpType, ActivationFunctionType
+    v, s, te, sy, S = g.vector, g.scalar, g.tensor, g.sync, T.sem
+    others = [d for d in range(N) if d != me]
+    mine = plan(core, T.cores, topo)
+    arrive = sum(len(plan(T.cores[r], T.cores, topo)[core]) for r in others)
+    leave = sum(len(e) for e in mine.values())
+    cnt = {"sv": 0, "sa": 0, "sg": 0, "st": 0, "sent": 0}
+
+    def note(ins, sem):
+        ins.then_inc(S[sem], 1)
+        cnt[sem] += 1
+        return cnt[sem]
+
+    def V(ins):
+        return note(ins, "sv")
+
+    def C(ins):
+        return note(ins, "sa")
+
+    def G(ins):
+        return note(ins, "sg")
+
+    def after(k=None):
+        v.wait_ge(S.sv, cnt["sv"] if k is None else k)
+
+    def W(ins):
+        return V(ins)
+
+    def send(sem, src, dst):
+        tr = []
+        for d in others:
+            rid, pid = topo.addr(T.cores[d], core)
+            tr.append(RemoteDMATransfer(dst_ids=[DstId(rid=rid, pnc=pid)], dma_engine_mask=sum(1 << e for e in mine[T.cores[d]]),
+                                        remote_sem=sem, src=src(d), dst=dst))
+        g.remote_dma_fused(tr, local_sem=S.sent)
+        cnt["sent"] += leave
+
+    def by(t):
+        return t.bitcast(dt.uint8)
+
+    def pick(eng, out, win, offs):
+        if eng is v:
+            return V(v.tensor_copy(out.bitcast(dt.uint32), win.bitcast(dt.uint32).indirect(offs)))
+        return C(s.activation(out, win.indirect(offs), F.Copy))
+
+    k_ew = V(v.memset(T.ew[:], -1))
+    g_val1 = G(g.iota(T.val1[:], [[1, 16], [16, 16]], 0, 0))
+    for q, qu in ((0, sy), (1, s)):
+        qu.wait_ge(S.sv, k_ew)
+        for k in (2 * q, 2 * q + 1):
+            qu.dma_start(T.ew[32 * k:32 * k + 16, 0:16], T.to[:, :]).then_inc(S.ld_e, 16)
+            qu.dma_start(T.ew[32 * k + 16:32 * k + 32, 16:32], T.to[:, :]).then_inc(S.ld_e, 16)
+    sy.dma_start(T.xb[:], T.x[:, :]).then_inc(S.ld_x, 16)
+    for q, qu in ((0, sy), (1, s)):
+        qu.wait_ge(S.sg, g_val1)
+        for k in range(4 * q, 4 * q + 4):
+            qu.dma_start(T.val1[16 * k + 1:16 * k + 2, :], T.to[:, :]).then_inc(S.ld_r, 16)
+    sy.dma_start(T.wb[:], T.w[:, :]).then_inc(S.ld_w, 16)
+
+    G(g.iota(T.part[:], [[1, 1]], 0, 1))
+    g_tti = G(g.iota(T.tti[:], [[-PK1, N], [16, LC]], 0, 0, allow_small_or_imprecise_dtypes=True))
+    g_val2 = G(g.iota(T.val2[:], [[1, N], [N, PK1]], 0, 0, allow_small_or_imprecise_dtypes=True))
+    k_zero = V(v.memset(T.zero[:], 0.0))
+    s.wait_ge(S.sv, k_zero)
+    for i in range(4):
+        c_win2 = C(s.activation(T.win2[:, 512 * i:512 * i + 512], T.zero[:], F.Identity, bias=NONE))
+    V(v.memset(T.restart[:], 1.0))
+    after()
+    V(v.memset(T.restart[:, 0::16], 0.0))
+    V(v.memset(T.ones[:], 1.0))
+    V(v.memset(T.win1[:], 0.0))
+    v.wait_ge(S.sg, g_tti)
+    V(v.tensor_scalar(T.par[:], T.part[:], 4, 1, A.logical_shift_right, A.bitwise_and))
+    V(v.tensor_scalar(T.low[:], T.part[:], 15, None, A.bitwise_and))
+    after()
+    V(v.tensor_copy(T.odd[:], T.par[:]))
+    V(v.tensor_scalar(T.even[:], T.par[:], -1.0, 1.0, A.mult, A.add))
+    V(v.tensor_scalar(T.odd8[:], T.par[:], 0.125, None, A.mult))
+    V(v.tensor_scalar(T.odd16[:], T.par[:], 16.0, None, A.mult))
+    V(v.tensor_copy(T.lowf[:], T.low[:]))
+    after()
+    V(v.tensor_scalar(T.tt[:], T.tti[:], T.lowf[:, 0:1], None, A.add))
+    V(v.memset(T.cn[:, 3:4], float(COLS)))
+    V(v.memset(T.eb[:], 0.0))
+    V(v.memset(T.cb[:, 0:10], 0))
+    V(v.memset(T.pb[:, 0:10], 0))
+    V(v.memset(T.xx[:, 0:5], 0.0))
+    V(v.memset(T.h1[:], 0.0))
+
+    v.wait_ge(S.ld_e, 16 * 8)
+    after()
+    V(v.tensor_scalar(T.ec[:], T.ew[:], 8, None, A.arith_shift_right))
+    after()
+    for q in range(N):
+        V(v.tensor_scalar(T.ind[:, 32 * q:32 * q + 32], T.ec[:], float(q), None, A.is_equal))
+    after()
+    V(v.transpose(T.indt[:], T.ind[:]))
+    after()
+    k = V(v.tensor_tensor_scan(T.cr[:], T.restart[:], T.indt[:], 0.0, A.mult, A.add))
+    V(v.tensor_copy(T.ind2[:], T.indt[:]))
+    after(k)
+    V(v.transpose(T.crt[:], T.cr[:]))
+    after()
+    V(v.tensor_tensor_scan(T.cum[:], T.ones[:], T.crt[:], 0.0, A.mult, A.add))
+    after()
+    k_z = V(v.transpose(T.z[:], T.cum[:]))
+    after()
+    V(v.tensor_tensor(T.ind2[:, 0::16], T.indt[:, 0::16], T.z[:, 15::16], A.subtract))
+    after()
+    V(v.tensor_tensor_scan(T.pp[:], T.restart[:], T.ind2[:], 0.0, A.mult, A.subtract))
+    after()
+    V(v.tensor_tensor(T.pm[:], T.pp[:], T.indt[:], A.mult))
+    after()
+    V(v.tensor_tensor(T.pm2[:], T.pm[:, 0:64], T.pm[:, 64:128], A.add))
+    after()
+    V(v.tensor_tensor(T.pm3[:], T.pm2[:, 0:32], T.pm2[:, 32:64], A.add))
+    after()
+    V(v.tensor_tensor(T.pos[:], T.pm3[:, 0:16], T.pm3[:, 16:32], A.add))
+    after()
+    k_s = V(v.tensor_scalar(T.si[:], T.pos[:], 0.25, -0.375, A.mult, A.add))
+    k_u = V(v.tensor_scalar(T.ui[:], T.pos[:], 1.0 / 64, -63.0 / 128, A.mult, A.add))
+    after(k_s)
+    k_t = V(v.tensor_scalar(T.t1[:], T.si[:], -511.0 / 128, T.odd8[:, 0:1], A.mult, A.add))
+    after(k_u)
+    V(v.tensor_scalar(T.t3[:], T.ui[:], 0.125, None, A.mult))
+    after(k_t)
+    V(v.tensor_tensor(T.t2[:], T.pos[:], T.t1[:], A.add))
+    after()
+    V(v.tensor_tensor(T.t4[:], T.t2[:], T.t3[:], A.add))
+    after()
+    V(v.tensor_scalar(T.off1[:], T.t4[:], 128.0, None, A.mult))
+    v.wait_ge(S.ld_r, 16 * 8)
+    after()
+    V(v.tensor_copy(T.win1[:, 0:512].indirect(T.off1[:, 0:16]), T.val1[:, 0:256]))
+    after()
+    V(v.transpose(T.wt1[:], T.win1[:]))
+    after()
+    V(v.tensor_tensor(T.l1f[:], T.wt1[:, 0::32], T.wt1[:, 16::32], A.add))
+    after()
+    V(v.tensor_copy(T.l1u[:], T.l1f[:]))
+    v.wait_ge(S.ld_x, 16)
+    k_l1 = V(v.quantize_mx(T.xq[:], T.xs[:], T.xb[:]))
+    after()
+    runs = [(a, b) for a, b in ((0, PK1 * me), (PK1 * (me + 1), COLS)) if a < b]
+    a1, b1 = PK1 * me, PK1 * (me + 1)
+    for a, b in runs:
+        k_p1 = pick(v, T.slot1q[:, a:b], T.xq[:], T.l1u[:, a // 16:b // 16])
+    pick(v, T.land1q[:, a1:b1], T.xq[:], T.l1u[:, a1 // 16:b1 // 16])
+
+    s.wait_ge(S.sv, k_z)
+    c = C(s.activation(T.cz[:], T.z[:, 31::32], F.Identity, scale=T.even[:, 0:1]))
+    s.wait_ge(S.sa, c)
+    for q in range(N - 1):
+        k_cn = C(s.activation(T.cn[:, q:q + 1], T.z[:, 32 * q + 15:32 * q + 16], F.Identity, bias=T.cz[:, q + 1:q + 2],
+                              scale=T.odd[:, 0:1]))
+    s.wait_ge(S.sa, k_cn)
+    k_cl = C(s.activation(T.cland[:, 8 * me:8 * me + 4], T.cn[:], F.Copy))
+    s.wait_ge(S.sv, k_l1)
+    for a, b in runs:
+        c_p1 = pick(s, T.slot1s[:, a:b], T.xs[:], T.l1u[:, a // 16:b // 16])
+    c_o1 = pick(s, T.land1s[:, a1:b1], T.xs[:], T.l1u[:, a1 // 16:b1 // 16])
+
+    g.wait_ge(S.sa, k_cn)
+    send(S.cnt, lambda d: T.cn[:], T.cland[:, 8 * me:8 * me + 4])
+    g.wait_ge(S.sv, k_p1)
+    send(S.p1c, lambda d: by(T.slot1q[:, PK1 * d:PK1 * (d + 1)]), by(T.land1q[:, a1:b1]))
+    g.wait_ge(S.sa, c_p1)
+    send(S.p1s, lambda d: T.slot1s[:, PK1 * d:PK1 * (d + 1)], T.land1s[:, a1:b1])
+
+    V(v.tensor_tensor(T.ts[:], T.wt1[:, 1::32], T.wt1[:, 17::32], A.add))
+    after()
+    V(v.tensor_scalar(T.hi[:], T.ts[:], 1.0 / 16, -15.0 / 32, A.mult, A.add))
+    after()
+    V(v.tensor_scalar(T.o1[:], T.hi[:], 16.0, T.odd16[:, 0:1], A.mult, A.add))
+    after()
+    V(v.tensor_tensor(T.o2[:], T.ts[:], T.o1[:], A.add))
+    after()
+    V(v.tensor_copy(T.off2[:], T.o2[:]))
+    v.wait_ge(S.sg, g_val2)
+    v.wait_ge(S.sa, c_win2)
+    after()
+    V(v.tensor_copy(T.win2[:, 0:2048].indirect(T.off2[:, 0:16]), T.val2[:, 0:256]))
+    after()
+    V(v.transpose(T.wt2[:], T.win2[:]))
+    after()
+    k_vo = V(v.tensor_tensor(T.vout[:], T.wt2[:, 0::32], T.wt2[:, 16::32], A.max))
+    g.wait_ge(S.sv, k_vo)
+    send(S.plc, lambda d: T.vout[:, 16 * d:16 * d + 16], T.vland[:, 16 * me:16 * me + 16])
+
+    v.wait_ge(S.cnt, arrive)
+    v.wait_ge(S.sa, k_cl)
+    for r in range(N):
+        V(v.tensor_copy(T.eb[:, 5 * r + 1:5 * r + 5], T.cland[:, 8 * r:8 * r + 4]))
+    after()
+    k = V(v.tensor_tensor(T.nn[:], T.eb[:, 1:21], T.eb[:, 0:20], A.subtract))
+    V(v.tensor_scalar(T.aa[:], T.eb[:, 0:20], 0.25, (N - 1 - me) / 4.0 - 0.375, A.mult, A.add))
+    after(k)
+    V(v.tensor_scalar(T.cb[:, 10:30], T.nn[:], 0.25, 0.375 - PK1, A.mult, A.add))
+    after()
+    V(v.tensor_tensor(T.pb[:, 10:30], T.cb[:, 5:25], T.cb[:, 0:20], A.add))
+    after()
+    V(v.tensor_tensor(T.sf[:], T.pb[:, 10:30], T.pb[:, 0:20], A.add))
+    after()
+    V(v.tensor_tensor(T.xx[:, 5:25], T.aa[:], T.sf[:], A.subtract))
+    after()
+    V(v.tensor_tensor(T.dd[:], T.xx[:, 5:25], T.xx[:, 0:20], A.subtract))
+    after()
+    for r in range(N):
+        for x, d in enumerate(others + [me]):
+            a = 21 * r + (LC * x if d != me else 16)
+            i = 5 * r + d
+            if r == 0:
+                V(v.tensor_scalar(T.h1[:, a:a + LC], T.tt[:, 0:LC], T.dd[:, i:i + 1], None, A.add))
+            else:
+                V(v.tensor_scalar(T.h1[:, a:a + LC], T.tt[:, LC * r:LC * r + LC], T.sf[:, i:i + 1], T.dd[:, i:i + 1],
+                                  A.is_ge, A.mult))
+    after()
+    V(v.tensor_tensor(T.h2[:], T.h1[:, 0:42], T.h1[:, 42:84], A.add))
+    after()
+    V(v.tensor_tensor(T.h3[:], T.h2[:, 0:21], T.h2[:, 21:42], A.add))
+    after()
+    k_l2 = V(v.tensor_scalar(T.l2u[:, 0:21], T.h3[:], float(COLS - 1), None, A.min))
+
+    own2 = slice(ST * me, ST * me + ST)
+    pk2 = slice(ST * me, ST * me + PK2)
+    v.wait_ge(S.p1c, arrive)
+    after()
+    k_p2 = pick(v, T.slot2q[:], T.land1q[:], T.l2u[:, 0:3 * LC])
+    pick(v, T.land2q[:, own2], T.land1q[:], T.l2u[:, 16:16 + LC])
+    s.wait_ge(S.sv, k_l2)
+    s.wait_ge(S.sa, c_o1)
+    s.wait_ge(S.p1s, arrive)
+    c_p2 = pick(s, T.slot2s[:], T.land1s[:], T.l2u[:, 0:3 * LC])
+    pick(s, T.land2s[:, own2], T.land1s[:], T.l2u[:, 16:16 + LC])
+    c_v = C(s.activation(T.vland[:, 16 * me:16 * me + 16], T.vout[:, 16 * me:16 * me + 16], F.Copy))
+    at = {d: slice(ST * x, ST * x + PK2) for x, d in enumerate(others)}
+    g.wait_ge(S.sv, k_p2)
+    send(S.p2c, lambda d: by(T.slot2q[:, at[d]]), by(T.land2q[:, pk2]))
+    g.wait_ge(S.sa, c_p2)
+    send(S.p2s, lambda d: T.slot2s[:, at[d]], T.land2s[:, pk2])
+
+    v.wait_ge(S.ld_w, 16)
+    V(v.quantize_mx(T.wq[:], T.ws[:], T.wb[:]))
+    k = V(v.tensor_scalar(T.s4[:], T.sf[:], 4.0, None, A.mult))
+    after(k)
+    V(v.tensor_tensor(T.cf[:], T.s4[:], T.eb[:, 0:20], A.subtract))
+    v.wait_ge(S.plc, arrive)
+    v.wait_ge(S.sa, c_v)
+    after()
+    k_vi = V(v.tensor_copy(T.vi[:], T.vland[:]))
+    for r in range(N):
+        k_k = V(v.tensor_scalar(T.kk[:, 16 * r:16 * r + 16], T.vland[:, 16 * r:16 * r + 16],
+                                T.cf[:, 5 * r + me:5 * r + me + 1], float(4 * PK1 * r), A.add, A.add))
+    after(k_vi)
+    k_m = V(v.tensor_scalar(T.m3[:], T.vi[:], 3, None, A.bitwise_and))
+    after(k_k)
+    V(v.tensor_scalar(T.ks[:], T.kk[:], 2, None, A.arith_shift_right))
+    after(k_m)
+    V(v.tensor_scalar(T.m80[:], T.m3[:], float(ST), None, A.mult))
+    after()
+    V(v.tensor_tensor(T.f1[:], T.m80[:], T.ks[:], A.add))
+    after()
+    V(v.tensor_tensor(T.f2[:], T.f1[:, 0:32], T.f1[:, 32:64], A.max))
+    after()
+    V(v.tensor_tensor(T.f3[:], T.f2[:, 0:16], T.f2[:, 16:32], A.max))
+    after()
+    k_fl = V(v.tensor_copy(T.flu[:], T.f3[:]))
+
+    v.wait_ge(S.p2c, arrive)
+    after()
+    s.wait_ge(S.sv, k_fl)
+    s.wait_ge(S.sa, cnt["sa"])
+    s.wait_ge(S.p2s, arrive)
+    H = COLS // 2
+    mm = {}
+    for h in range(2):
+        part = slice(H * h, H * h + H)
+        te.wait_ge(S.sv, pick(v, T.finq[:, part], T.land2q[:], T.flu[:, 8 * h:8 * h + 8]))
+        te.wait_ge(S.sa, pick(s, T.fins[:, part], T.land2s[:], T.flu[:, 8 * h:8 * h + 8]))
+        for o in range(O):
+            b = 512 * (2 * h + o)
+            mm[h, o] = note(te.matmul_mx(T.ps[:, b:b + H], T.wq[:, 128 * o:128 * o + 128], T.ws[:, 128 * o:128 * o + 128],
+                                         T.finq[:, part], T.fins[:, part], True, True), "st")
+    for h in range(2):
+        b = 1024 * h
+        v.wait_ge(S.st, mm[h, 0])
+        V(v.tensor_copy(T.yb[:, H * h:H * h + H], T.ps[:, b:b + H]))
+        s.wait_ge(S.st, mm[h, 1])
+        C(s.activation(T.yb[:, COLS + H * h:COLS + H * h + H], T.ps[:, b + 512:b + 512 + H], F.Copy))
+    sy.wait_ge(S.sv, cnt["sv"])
+    sy.dma_start(T.y[:, 0:COLS], T.yb[:, 0:COLS]).then_inc(S.yo0, 16)
+    s.wait_ge(S.sa, cnt["sa"])
+    s.dma_start(T.y[:, COLS:2 * COLS], T.yb[:, COLS:2 * COLS]).then_inc(S.yo1, 16)
+    sy.wait_ge(S.yo0, 16)
+    s.wait_ge(S.yo1, 16)
+    g.wait_ge(S.sent, cnt["sent"])
+    g.wait_ge(S.sg, cnt["sg"])

@@ -6,24 +6,25 @@ PK1 = COLS // N
 PK2 = COLS // N + N - 1
 ST = 80
 LC = ST // 16
+W1, W2 = COLS + 32, N * COLS + 32
 NONE = -8192.0
-
 BUFFERS = {
     "float8_e4m3fn_x4": "xq 256 wq 256 slot1q 256 land1q 256 slot2q 240 land2q 320 finq 256",
     "uint8": "xs 256 ws 256 slot1s 256 land1s 256 slot2s 240 land2s 320 fins 256",
     "bfloat16": "xb 1024 wb 1024 restart 128 ones 128 val2 256 ind 128 indt 128 ind2 128 cr 128 crt 128 cum 128 z 128 pp 128 "
-                "pm 128 pm2 64 pm3 32 win2 2048 wt2 2048 vout 64 vland 64 cn 4 cland 32",
-    "float32": "odd 1 even 1 odd8 1 odd16 1 lowf 1 tti 20 tt 20 pos 16 t1 16 t2 16 t3 16 t4 16 win1 512 wt1 512 l1f 16 ts 16 "
-               "o1 16 o2 16 cz 4 eb 21 nn 20 sf 20 xx 25 dd 20 h1 84 h2 42 h3 21 s4 20 cf 20 f1 64 f2 32 f3 16 yb 512 zero 512",
-    "int32": "part 1 par 1 low 1 val1 256 ew 32 ec 32 si 16 ui 16 hi 16 cb 30 aa 20 pb 30 vi 64 m3 64 m80 64 kk 64 ks 64",
-    "uint16": "off1 16 l1u 16 off2 16 l2u 22 flu 16",
+                "pm 128 pm2 64 pm3 32 win2 1056 wt2 1056 vout 64 vland 64 cn 4 cland 32",
+    "float32": "odd 1 even 1 odd4 1 odd16 1 lowf 1 lows 1 tti 20 tt 20 pos 16 t1 16 t2 16 win1 288 wt1 288 selm 1 selb 1 selk 4 "
+               "self 4 tsf 16 cz 4 eb 21 nn 20 sf 20 xx 25 dd 20 h1 60 h2 30 h3 15 g1 20 g2 10 g3 5 s4 20 cf 20 f1 64 f2 32 f3 16 "
+               "yb 512",
+    "int32": "part 1 par 1 low 1 bit 1 val1 256 ew 32 ec 32 si 16 cb 30 aa 20 pb 30 vi 64 m3 64 m80 64 kk 64 ks 64",
+    "uint16": "off1 16 l1u 16 off2 16 l2u 16 lou 6 flu 16 sel 4 selr 4",
 }
 SCRATCH = {"ps": ("psum", [128, 2048], "float32")}
 for _t, _l in BUFFERS.items():
     _w = _l.split()
     for _n, _c in zip(_w[0::2], _w[1::2]):
         SCRATCH[_n] = ("sbuf", [128, int(_c)], _t)
-SEMAPHORES = "sv sa sg st ld_e ld_x ld_r ld_w cnt p1c p1s plc p2c p2s sent yo0 yo1".split()
+SEMAPHORES = "sv sa sg st ld_e ld_x ld_r ld_w cnt p1c p1s plc p2c p2s sent yo".split()
 
 
 def plan(src, cores, topo):
@@ -46,299 +47,280 @@ def rank_program(g, core, T, topo):
     if me is None:
         return
     A, F = AluOpType, ActivationFunctionType
-    v, s, te, sy, S = g.vector, g.scalar, g.tensor, g.sync, T.sem
+    S = T.sem
     others = [d for d in range(N) if d != me]
     mine = plan(core, T.cores, topo)
     arrive = sum(len(plan(T.cores[r], T.cores, topo)[core]) for r in others)
     leave = sum(len(e) for e in mine.values())
-    cnt = {"sv": 0, "sa": 0, "sg": 0, "st": 0, "sent": 0}
+    v, s, te, sy = g.vector, g.scalar, g.tensor, g.sync
+    own_sem = {"v": "sv", "s": "sa", "g": "sg", "t": "st"}
+    queue = {"v": v, "s": s, "g": g, "t": te, "y": sy}
+    cnt = {k: 0 for k in SEMAPHORES}
+    made = {}
+    seen = {}
 
-    def note(ins, sem):
-        ins.then_inc(S[sem], 1)
-        cnt[sem] += 1
-        return cnt[sem]
+    def hold(q, sem, k):
+        if seen.get((q, sem), 0) < k:
+            queue[q].wait_ge(S[sem], k)
+            seen[q, sem] = k
 
-    def V(ins):
-        return note(ins, "sv")
+    def need(q, *names):
+        for n in names:
+            for sem, k in made.get(n, {}).items():
+                hold(q, sem, k)
 
-    def C(ins):
-        return note(ins, "sa")
+    def ap(x):
+        return T[x][:] if not isinstance(x, tuple) else T[x[0]][:, slice(*x[1:])]
 
-    def G(ins):
-        return note(ins, "sg")
+    def name(x):
+        return x[0] if isinstance(x, tuple) else x
 
-    def after(k=None):
-        v.wait_ge(S.sv, cnt["sv"] if k is None else k)
+    def named(*xs):
+        return [name(x) for x in xs if isinstance(x, (str, tuple))]
 
-    def W(ins):
-        return V(ins)
+    def done(q, ins, out, sem=None, by=1):
+        sem = sem or own_sem[q]
+        ins.then_inc(S[sem], by)
+        cnt[sem] += by
+        for o in out:
+            made.setdefault(name(o), {})[sem] = cnt[sem]
 
-    def send(sem, src, dst):
-        tr = []
+    def cp(out, i, q="v"):
+        need(q, name(i))
+        done(q, v.tensor_copy(ap(out), ap(i)) if q == "v" else s.activation(ap(out), ap(i), F.Copy), [out])
+
+    def tt(out, a, b, op):
+        need("v", name(a), name(b))
+        done("v", v.tensor_tensor(ap(out), ap(a), ap(b), op), [out])
+
+    def ts(out, a, s1, op, s2=None, op2=None):
+        need("v", *named(a, s1, s2))
+        s1, s2 = [ap(k) if isinstance(k, (str, tuple)) else k for k in (s1, s2)]
+        done("v", v.tensor_scalar(ap(out), ap(a), s1, s2, op, op2) if op2 else v.tensor_scalar(ap(out), ap(a), s1, None, op), [out])
+
+    def tr(out, i):
+        need("v", i)
+        done("v", v.transpose(ap(out), ap(i)), [out])
+
+    def scan(out, a, b, op):
+        need("v", a, b)
+        done("v", v.tensor_tensor_scan(ap(out), ap(a), ap(b), 0.0, A.mult, op), [out])
+
+    def fill(x, c):
+        done("v", v.memset(ap(x), c), [x])
+
+    def iota(out, pat, base=0, cm=0, whole=False):
+        kw = {} if whole else {"allow_small_or_imprecise_dtypes": True}
+        done("g", g.iota(ap(out), pat, base, cm, **kw), [out])
+
+    def act(out, i, offs=None, **kw):
+        need("s", *named(i, offs, *kw.values()))
+        kw = {k: ap(x) if isinstance(x, (str, tuple)) else x for k, x in kw.items()}
+        done("s", s.activation(ap(out), ap(i) if offs is None else ap(i).indirect(ap(offs)), F.Identity, **kw), [out])
+
+    def load(q, out, src, sem):
+        done(q, queue[q].dma_start(ap(out), src), [out], sem, 16)
+
+    def quant(k):
+        need("v", k + "b")
+        done("v", v.quantize_mx(ap(k + "q"), ap(k + "s"), ap(k + "b")), [k + "q", k + "s"])
+
+    def pick(q, out, win, offs):
+        need(q, win, name(offs))
+        if name(out)[-1] == "q":
+            done(q, v.tensor_copy(ap(out).bitcast(dt.uint32), ap(win).bitcast(dt.uint32).indirect(ap(offs))), [out])
+        elif q == "v":
+            done(q, v.tensor_copy(ap(out), ap(win).indirect(ap(offs))), [out])
+        else:
+            done(q, s.activation(ap(out), ap(win).indirect(ap(offs)), F.Copy), [out])
+
+    def send(sem, buf, dst, cut, codes=False):
+        need("g", buf)
+        raw = (lambda t: t.bitcast(dt.uint8)) if codes else (lambda t: t)
+        tl = []
         for d in others:
             rid, pid = topo.addr(T.cores[d], core)
-            tr.append(RemoteDMATransfer(dst_ids=[DstId(rid=rid, pnc=pid)], dma_engine_mask=sum(1 << e for e in mine[T.cores[d]]),
-                                        remote_sem=sem, src=src(d), dst=dst))
-        g.remote_dma_fused(tr, local_sem=S.sent)
+            tl.append(RemoteDMATransfer(dst_ids=[DstId(rid=rid, pnc=pid)], dma_engine_mask=sum(1 << e for e in mine[T.cores[d]]),
+                                        remote_sem=S[sem], src=raw(ap((buf,) + cut(d))), dst=raw(ap(dst))))
+        g.remote_dma_fused(tl, local_sem=S.sent)
         cnt["sent"] += leave
+        made.setdefault(name(dst), {})[sem] = arrive
 
-    def by(t):
-        return t.bitcast(dt.uint8)
+    fill("ew", -1)
+    k_ew = cnt["sv"]
+    iota("part", [[1, 1]], 0, 1, True)
+    iota("val1", [[1, 16], [16, 16]], 0, 0, True)
+    k_val = cnt["sg"]
+    for q, k0 in (("y", 0), ("s", 2)):
+        hold(q, "sv", k_ew)
+        for k in (k0, k0 + 1):
+            for a in (0, 16):
+                done(q, queue[q].dma_start(T.ew[32 * k + a:32 * k + a + 16, a:a + 16], T.to[:, :]), ["ew"], "ld_e", 16)
+    for q, k0 in (("y", 0), ("s", 4)):
+        hold(q, "sg", k_val)
+        for k in range(k0, k0 + 4):
+            done(q, queue[q].dma_start(T.val1[16 * k + 1:16 * k + 2, :], T.to[:, :]), ["val1"], "ld_r", 16)
+    load("y", "xb", T.x[:, :], "ld_x")
+    load("y", "wb", T.w[:, :], "ld_w")
 
-    def pick(eng, out, win, offs):
-        if eng is v:
-            return V(v.tensor_copy(out.bitcast(dt.uint32), win.bitcast(dt.uint32).indirect(offs)))
-        return C(s.activation(out, win.indirect(offs), F.Copy))
+    fill("win1", 0.0)
+    act("restart", ("win1", 0, 128), bias=1.0)
+    act("ones", ("win1", 0, 128), bias=1.0)
+    need("s", "restart")
+    act(("restart", 0, 128, 16), ("win1", 0, 8))
+    for a in range(0, W2, W1):
+        n = min(W1, W2 - a)
+        act(("win2", a, a + n), ("win1", 0, n), bias=NONE)
+    act("eb", ("win1", 0, 21))
+    act(("cn", 3, 4), ("win1", 0, 1), bias=float(COLS))
+    act(("xx", 0, 5), ("win1", 0, 5))
+    need("s", "eb")
+    act(("eb", 4, 20, 5), ("win1", 0, 4), bias=float(COLS))
+    k_zero = cnt["sa"]
+    iota("selk", [[16 * 16, 4]])
+    iota("tti", [[-PK1, N], [16, LC]])
+    iota(("cb", 0, 10), [[0, 10]], 0, 0, True)
+    iota(("pb", 0, 10), [[0, 10]], 0, 0, True)
+    iota("val2", [[1, N], [N, PK1]])
+    ts("par", "part", 4, A.logical_shift_right, 1, A.bitwise_and)
+    ts("low", "part", 15, A.bitwise_and)
+    ts("bit", "part", 1, A.bitwise_and)
+    cp("odd", "par")
+    ts("even", "par", -1.0, A.mult, 1.0, A.add)
+    ts("odd4", "par", 0.25, A.mult)
+    ts("odd16", "par", 16.0, A.mult)
+    ts("selm", "par", -64.0, A.mult, 32.0, A.add)
+    cp("lowf", "low")
+    ts("selb", "bit", ("selm", 0, 1), A.mult, ("odd16", 0, 1), A.add)
+    ts("tt", "tti", ("lowf", 0, 1), A.add)
+    ts("lows", "low", 16.0, A.mult, ("selb", 0, 1), A.add)
+    ts("self", "selk", ("lows", 0, 1), A.add)
+    cp("sel", "self")
+    ts("selr", "self", 1.0, A.add)
 
-    k_ew = V(v.memset(T.ew[:], -1))
-    g_val1 = G(g.iota(T.val1[:], [[1, 16], [16, 16]], 0, 0))
-    for q, qu in ((0, sy), (1, s)):
-        qu.wait_ge(S.sv, k_ew)
-        for k in (2 * q, 2 * q + 1):
-            qu.dma_start(T.ew[32 * k:32 * k + 16, 0:16], T.to[:, :]).then_inc(S.ld_e, 16)
-            qu.dma_start(T.ew[32 * k + 16:32 * k + 32, 16:32], T.to[:, :]).then_inc(S.ld_e, 16)
-    sy.dma_start(T.xb[:], T.x[:, :]).then_inc(S.ld_x, 16)
-    for q, qu in ((0, sy), (1, s)):
-        qu.wait_ge(S.sg, g_val1)
-        for k in range(4 * q, 4 * q + 4):
-            qu.dma_start(T.val1[16 * k + 1:16 * k + 2, :], T.to[:, :]).then_inc(S.ld_r, 16)
-    sy.dma_start(T.wb[:], T.w[:, :]).then_inc(S.ld_w, 16)
-
-    G(g.iota(T.part[:], [[1, 1]], 0, 1))
-    g_tti = G(g.iota(T.tti[:], [[-PK1, N], [16, LC]], 0, 0, allow_small_or_imprecise_dtypes=True))
-    g_val2 = G(g.iota(T.val2[:], [[1, N], [N, PK1]], 0, 0, allow_small_or_imprecise_dtypes=True))
-    k_zero = V(v.memset(T.zero[:], 0.0))
-    s.wait_ge(S.sv, k_zero)
-    for i in range(4):
-        c_win2 = C(s.activation(T.win2[:, 512 * i:512 * i + 512], T.zero[:], F.Identity, bias=NONE))
-    V(v.memset(T.restart[:], 1.0))
-    after()
-    V(v.memset(T.restart[:, 0::16], 0.0))
-    V(v.memset(T.ones[:], 1.0))
-    V(v.memset(T.win1[:], 0.0))
-    v.wait_ge(S.sg, g_tti)
-    V(v.tensor_scalar(T.par[:], T.part[:], 4, 1, A.logical_shift_right, A.bitwise_and))
-    V(v.tensor_scalar(T.low[:], T.part[:], 15, None, A.bitwise_and))
-    after()
-    V(v.tensor_copy(T.odd[:], T.par[:]))
-    V(v.tensor_scalar(T.even[:], T.par[:], -1.0, 1.0, A.mult, A.add))
-    V(v.tensor_scalar(T.odd8[:], T.par[:], 0.125, None, A.mult))
-    V(v.tensor_scalar(T.odd16[:], T.par[:], 16.0, None, A.mult))
-    V(v.tensor_copy(T.lowf[:], T.low[:]))
-    after()
-    V(v.tensor_scalar(T.tt[:], T.tti[:], T.lowf[:, 0:1], None, A.add))
-    V(v.memset(T.cn[:, 3:4], float(COLS)))
-    V(v.memset(T.eb[:], 0.0))
-    V(v.memset(T.cb[:, 0:10], 0))
-    V(v.memset(T.pb[:, 0:10], 0))
-    V(v.memset(T.xx[:, 0:5], 0.0))
-    V(v.memset(T.h1[:], 0.0))
-
-    v.wait_ge(S.ld_e, 16 * 8)
-    after()
-    V(v.tensor_scalar(T.ec[:], T.ew[:], 8, None, A.arith_shift_right))
-    after()
+    ts("ec", "ew", 8, A.arith_shift_right)
     for q in range(N):
-        V(v.tensor_scalar(T.ind[:, 32 * q:32 * q + 32], T.ec[:], float(q), None, A.is_equal))
-    after()
-    V(v.transpose(T.indt[:], T.ind[:]))
-    after()
-    k = V(v.tensor_tensor_scan(T.cr[:], T.restart[:], T.indt[:], 0.0, A.mult, A.add))
-    V(v.tensor_copy(T.ind2[:], T.indt[:]))
-    after(k)
-    V(v.transpose(T.crt[:], T.cr[:]))
-    after()
-    V(v.tensor_tensor_scan(T.cum[:], T.ones[:], T.crt[:], 0.0, A.mult, A.add))
-    after()
-    k_z = V(v.transpose(T.z[:], T.cum[:]))
-    after()
-    V(v.tensor_tensor(T.ind2[:, 0::16], T.indt[:, 0::16], T.z[:, 15::16], A.subtract))
-    after()
-    V(v.tensor_tensor_scan(T.pp[:], T.restart[:], T.ind2[:], 0.0, A.mult, A.subtract))
-    after()
-    V(v.tensor_tensor(T.pm[:], T.pp[:], T.indt[:], A.mult))
-    after()
-    V(v.tensor_tensor(T.pm2[:], T.pm[:, 0:64], T.pm[:, 64:128], A.add))
-    after()
-    V(v.tensor_tensor(T.pm3[:], T.pm2[:, 0:32], T.pm2[:, 32:64], A.add))
-    after()
-    V(v.tensor_tensor(T.pos[:], T.pm3[:, 0:16], T.pm3[:, 16:32], A.add))
-    after()
-    k_s = V(v.tensor_scalar(T.si[:], T.pos[:], 0.25, -0.375, A.mult, A.add))
-    k_u = V(v.tensor_scalar(T.ui[:], T.pos[:], 1.0 / 64, -63.0 / 128, A.mult, A.add))
-    after(k_s)
-    k_t = V(v.tensor_scalar(T.t1[:], T.si[:], -511.0 / 128, T.odd8[:, 0:1], A.mult, A.add))
-    after(k_u)
-    V(v.tensor_scalar(T.t3[:], T.ui[:], 0.125, None, A.mult))
-    after(k_t)
-    V(v.tensor_tensor(T.t2[:], T.pos[:], T.t1[:], A.add))
-    after()
-    V(v.tensor_tensor(T.t4[:], T.t2[:], T.t3[:], A.add))
-    after()
-    V(v.tensor_scalar(T.off1[:], T.t4[:], 128.0, None, A.mult))
-    v.wait_ge(S.ld_r, 16 * 8)
-    after()
-    V(v.tensor_copy(T.win1[:, 0:512].indirect(T.off1[:, 0:16]), T.val1[:, 0:256]))
-    after()
-    V(v.transpose(T.wt1[:], T.win1[:]))
-    after()
-    V(v.tensor_tensor(T.l1f[:], T.wt1[:, 0::32], T.wt1[:, 16::32], A.add))
-    after()
-    V(v.tensor_copy(T.l1u[:], T.l1f[:]))
-    v.wait_ge(S.ld_x, 16)
-    k_l1 = V(v.quantize_mx(T.xq[:], T.xs[:], T.xb[:]))
-    after()
+        ts(("ind", 32 * q, 32 * q + 32), "ec", float(q), A.is_equal)
+    tr("indt", "ind")
+    scan("cr", "restart", "indt", A.add)
+    cp("ind2", "indt")
+    tr("crt", "cr")
+    scan("cum", "ones", "crt", A.add)
+    tr("z", "cum")
+    tt(("ind2", 0, 128, 16), ("indt", 0, 128, 16), ("z", 15, 128, 16), A.subtract)
+    scan("pp", "restart", "ind2", A.subtract)
+    tt("pm", "pp", "indt", A.mult)
+    tt("pm2", ("pm", 0, 64), ("pm", 64, 128), A.add)
+    tt("pm3", ("pm2", 0, 32), ("pm2", 32, 64), A.add)
+    tt("pos", ("pm3", 0, 16), ("pm3", 16, 32), A.add)
+    ts("si", "pos", 0.25, A.mult, -0.375, A.add)
+    ts("t1", "si", -(4.0 * PK1 - 1) / PK1, A.mult, ("odd4", 0, 1), A.add)
+    tt("t2", "pos", "t1", A.add)
+    ts("off1", "t2", float(PK1), A.mult)
+    need("v", "val1", "off1", "win1")
+    hold("v", "sa", k_zero)
+    done("v", v.tensor_copy(T.win1[:, 0:W1].indirect(T.off1[:, 0:16]), T.val1[:, 0:COLS]), ["win1"])
+    tr("wt1", "win1")
+    quant("x")
+    need("v", "wt1", "sel")
+    done("v", v.tensor_copy(T.l1u[:], T.wt1[:, 0:W1].indirect(T.sel[:, 0:1])), ["l1u"])
     runs = [(a, b) for a, b in ((0, PK1 * me), (PK1 * (me + 1), COLS)) if a < b]
     a1, b1 = PK1 * me, PK1 * (me + 1)
     for a, b in runs:
-        k_p1 = pick(v, T.slot1q[:, a:b], T.xq[:], T.l1u[:, a // 16:b // 16])
-    pick(v, T.land1q[:, a1:b1], T.xq[:], T.l1u[:, a1 // 16:b1 // 16])
+        pick("v", ("slot1q", a, b), "xq", ("l1u", a // 16, b // 16))
+    pick("v", ("land1q", a1, b1), "xq", ("l1u", a1 // 16, b1 // 16))
 
-    s.wait_ge(S.sv, k_z)
-    c = C(s.activation(T.cz[:], T.z[:, 31::32], F.Identity, scale=T.even[:, 0:1]))
-    s.wait_ge(S.sa, c)
+    act("cz", ("z", 31, 128, 32), scale=("even", 0, 1))
     for q in range(N - 1):
-        k_cn = C(s.activation(T.cn[:, q:q + 1], T.z[:, 32 * q + 15:32 * q + 16], F.Identity, bias=T.cz[:, q + 1:q + 2],
-                              scale=T.odd[:, 0:1]))
-    s.wait_ge(S.sa, k_cn)
-    k_cl = C(s.activation(T.cland[:, 8 * me:8 * me + 4], T.cn[:], F.Copy))
-    s.wait_ge(S.sv, k_l1)
+        act(("cn", q, q + 1), ("z", 32 * q + 15, 32 * q + 16), bias=("cz", q + 1, q + 2), scale=("odd", 0, 1))
+    cp(("cland", 8 * me, 8 * me + 4), "cn", "s")
     for a, b in runs:
-        c_p1 = pick(s, T.slot1s[:, a:b], T.xs[:], T.l1u[:, a // 16:b // 16])
-    c_o1 = pick(s, T.land1s[:, a1:b1], T.xs[:], T.l1u[:, a1 // 16:b1 // 16])
+        pick("s", ("slot1s", a, b), "xs", ("l1u", a // 16, b // 16))
+    act("tsf", "wt1", ("selr", 0, 1), bias=("odd16", 0, 1))
+    pick("s", ("land1s", a1, b1), "xs", ("l1u", a1 // 16, b1 // 16))
 
-    g.wait_ge(S.sa, k_cn)
-    send(S.cnt, lambda d: T.cn[:], T.cland[:, 8 * me:8 * me + 4])
-    g.wait_ge(S.sv, k_p1)
-    send(S.p1c, lambda d: by(T.slot1q[:, PK1 * d:PK1 * (d + 1)]), by(T.land1q[:, a1:b1]))
-    g.wait_ge(S.sa, c_p1)
-    send(S.p1s, lambda d: T.slot1s[:, PK1 * d:PK1 * (d + 1)], T.land1s[:, a1:b1])
+    send("cnt", "cn", ("cland", 8 * me, 8 * me + 4), lambda d: (0, 4))
+    cut1 = lambda d: (PK1 * d, PK1 * (d + 1))
+    send("p1c", "slot1q", ("land1q", a1, b1), cut1, True)
+    send("p1s", "slot1s", ("land1s", a1, b1), cut1)
 
-    V(v.tensor_tensor(T.ts[:], T.wt1[:, 1::32], T.wt1[:, 17::32], A.add))
-    after()
-    V(v.tensor_scalar(T.hi[:], T.ts[:], 1.0 / 16, -15.0 / 32, A.mult, A.add))
-    after()
-    V(v.tensor_scalar(T.o1[:], T.hi[:], 16.0, T.odd16[:, 0:1], A.mult, A.add))
-    after()
-    V(v.tensor_tensor(T.o2[:], T.ts[:], T.o1[:], A.add))
-    after()
-    V(v.tensor_copy(T.off2[:], T.o2[:]))
-    v.wait_ge(S.sg, g_val2)
-    v.wait_ge(S.sa, c_win2)
-    after()
-    V(v.tensor_copy(T.win2[:, 0:2048].indirect(T.off2[:, 0:16]), T.val2[:, 0:256]))
-    after()
-    V(v.transpose(T.wt2[:], T.win2[:]))
-    after()
-    k_vo = V(v.tensor_tensor(T.vout[:], T.wt2[:, 0::32], T.wt2[:, 16::32], A.max))
-    g.wait_ge(S.sv, k_vo)
-    send(S.plc, lambda d: T.vout[:, 16 * d:16 * d + 16], T.vland[:, 16 * me:16 * me + 16])
+    cp("off2", "tsf")
+    need("v", "val2", "off2", "win2")
+    done("v", v.tensor_copy(T.win2[:, 0:W2].indirect(T.off2[:, 0:16]), T.val2[:, 0:COLS]), ["win2"])
+    tr("wt2", "win2")
+    for q in range(N - 1):
+        cp(("eb", q + 1, 20, 5), ("cland", q, 32, 8), "s")
+    act("vout", "wt2", "sel")
+    send("plc", "vout", ("vland", 16 * me, 16 * me + 16), lambda d: (16 * d, 16 * d + 16))
 
-    v.wait_ge(S.cnt, arrive)
-    v.wait_ge(S.sa, k_cl)
+    tt("nn", ("eb", 1, 21), ("eb", 0, 20), A.subtract)
+    ts("aa", ("eb", 0, 20), 0.25, A.mult, (N - 1 - me) / 4.0 - 0.375, A.add)
+    ts(("cb", 10, 30), "nn", 0.25, A.mult, 0.375 - PK1, A.add)
+    tt(("pb", 10, 30), ("cb", 5, 25), ("cb", 0, 20), A.add)
+    tt("sf", ("pb", 10, 30), ("pb", 0, 20), A.add)
+    tt(("xx", 5, 25), "aa", "sf", A.subtract)
+    tt("dd", ("xx", 5, 25), ("xx", 0, 20), A.subtract)
+
+    def steps(dests, b1, b2, b3, lst):
+        n = LC * len(dests)
+        for r in range(N):
+            for x, d in enumerate(dests):
+                o, i = (b1, n * r + LC * x, n * r + LC * x + LC), 5 * r + d
+                if r == 0:
+                    ts(o, ("tt", 0, LC), ("dd", i, i + 1), A.add)
+                else:
+                    ts(o, ("tt", LC * r, LC * r + LC), ("sf", i, i + 1), A.is_ge, ("dd", i, i + 1), A.mult)
+        tt(b2, (b1, 0, 2 * n), (b1, 2 * n, 4 * n), A.add)
+        tt(b3, (b2, 0, n), (b2, n, 2 * n), A.add)
+        ts((lst, 0, n), b3, float(COLS - 1), A.min)
+
+    own2 = (ST * me, ST * me + ST)
+    pk2 = (ST * me, ST * me + PK2)
+    steps(others, "h1", "h2", "h3", "l2u")
+    pick("v", "slot2q", "land1q", ("l2u", 0, 3 * LC))
+    steps([me], "g1", "g2", "g3", "lou")
+    pick("v", ("land2q",) + own2, "land1q", ("lou", 0, LC))
+    pick("s", "slot2s", "land1s", ("l2u", 0, 3 * LC))
+    cp(("vland", 16 * me, 16 * me + 16), ("vout", 16 * me, 16 * me + 16), "s")
+    pick("s", ("land2s",) + own2, "land1s", ("lou", 0, LC))
+    cut2 = lambda d: (ST * others.index(d), ST * others.index(d) + PK2)
+    send("p2c", "slot2q", ("land2q",) + pk2, cut2, True)
+    send("p2s", "slot2s", ("land2s",) + pk2, cut2)
+
+    quant("w")
+    ts("s4", "sf", 4.0, A.mult)
+    tt("cf", "s4", ("eb", 0, 20), A.subtract)
+    cp("vi", "vland")
     for r in range(N):
-        V(v.tensor_copy(T.eb[:, 5 * r + 1:5 * r + 5], T.cland[:, 8 * r:8 * r + 4]))
-    after()
-    k = V(v.tensor_tensor(T.nn[:], T.eb[:, 1:21], T.eb[:, 0:20], A.subtract))
-    V(v.tensor_scalar(T.aa[:], T.eb[:, 0:20], 0.25, (N - 1 - me) / 4.0 - 0.375, A.mult, A.add))
-    after(k)
-    V(v.tensor_scalar(T.cb[:, 10:30], T.nn[:], 0.25, 0.375 - PK1, A.mult, A.add))
-    after()
-    V(v.tensor_tensor(T.pb[:, 10:30], T.cb[:, 5:25], T.cb[:, 0:20], A.add))
-    after()
-    V(v.tensor_tensor(T.sf[:], T.pb[:, 10:30], T.pb[:, 0:20], A.add))
-    after()
-    V(v.tensor_tensor(T.xx[:, 5:25], T.aa[:], T.sf[:], A.subtract))
-    after()
-    V(v.tensor_tensor(T.dd[:], T.xx[:, 5:25], T.xx[:, 0:20], A.subtract))
-    after()
-    for r in range(N):
-        for x, d in enumerate(others + [me]):
-            a = 21 * r + (LC * x if d != me else 16)
-            i = 5 * r + d
-            if r == 0:
-                V(v.tensor_scalar(T.h1[:, a:a + LC], T.tt[:, 0:LC], T.dd[:, i:i + 1], None, A.add))
-            else:
-                V(v.tensor_scalar(T.h1[:, a:a + LC], T.tt[:, LC * r:LC * r + LC], T.sf[:, i:i + 1], T.dd[:, i:i + 1],
-                                  A.is_ge, A.mult))
-    after()
-    V(v.tensor_tensor(T.h2[:], T.h1[:, 0:42], T.h1[:, 42:84], A.add))
-    after()
-    V(v.tensor_tensor(T.h3[:], T.h2[:, 0:21], T.h2[:, 21:42], A.add))
-    after()
-    k_l2 = V(v.tensor_scalar(T.l2u[:, 0:21], T.h3[:], float(COLS - 1), None, A.min))
+        ts(("kk", 16 * r, 16 * r + 16), ("vland", 16 * r, 16 * r + 16), ("cf", 5 * r + me, 5 * r + me + 1), A.add,
+           float(4 * PK1 * r), A.add)
+    ts("m3", "vi", 3, A.bitwise_and)
+    ts("ks", "kk", 2, A.arith_shift_right)
+    ts("m80", "m3", float(ST), A.mult)
+    tt("f1", "m80", "ks", A.add)
+    tt("f2", ("f1", 0, 32), ("f1", 32, 64), A.max)
+    tt("f3", ("f2", 0, 16), ("f2", 16, 32), A.max)
+    cp("flu", "f3")
 
-    own2 = slice(ST * me, ST * me + ST)
-    pk2 = slice(ST * me, ST * me + PK2)
-    v.wait_ge(S.p1c, arrive)
-    after()
-    k_p2 = pick(v, T.slot2q[:], T.land1q[:], T.l2u[:, 0:3 * LC])
-    pick(v, T.land2q[:, own2], T.land1q[:], T.l2u[:, 16:16 + LC])
-    s.wait_ge(S.sv, k_l2)
-    s.wait_ge(S.sa, c_o1)
-    s.wait_ge(S.p1s, arrive)
-    c_p2 = pick(s, T.slot2s[:], T.land1s[:], T.l2u[:, 0:3 * LC])
-    pick(s, T.land2s[:, own2], T.land1s[:], T.l2u[:, 16:16 + LC])
-    c_v = C(s.activation(T.vland[:, 16 * me:16 * me + 16], T.vout[:, 16 * me:16 * me + 16], F.Copy))
-    at = {d: slice(ST * x, ST * x + PK2) for x, d in enumerate(others)}
-    g.wait_ge(S.sv, k_p2)
-    send(S.p2c, lambda d: by(T.slot2q[:, at[d]]), by(T.land2q[:, pk2]))
-    g.wait_ge(S.sa, c_p2)
-    send(S.p2s, lambda d: T.slot2s[:, at[d]], T.land2s[:, pk2])
-
-    v.wait_ge(S.ld_w, 16)
-    V(v.quantize_mx(T.wq[:], T.ws[:], T.wb[:]))
-    k = V(v.tensor_scalar(T.s4[:], T.sf[:], 4.0, None, A.mult))
-    after(k)
-    V(v.tensor_tensor(T.cf[:], T.s4[:], T.eb[:, 0:20], A.subtract))
-    v.wait_ge(S.plc, arrive)
-    v.wait_ge(S.sa, c_v)
-    after()
-    k_vi = V(v.tensor_copy(T.vi[:], T.vland[:]))
-    for r in range(N):
-        k_k = V(v.tensor_scalar(T.kk[:, 16 * r:16 * r + 16], T.vland[:, 16 * r:16 * r + 16],
-                                T.cf[:, 5 * r + me:5 * r + me + 1], float(4 * PK1 * r), A.add, A.add))
-    after(k_vi)
-    k_m = V(v.tensor_scalar(T.m3[:], T.vi[:], 3, None, A.bitwise_and))
-    after(k_k)
-    V(v.tensor_scalar(T.ks[:], T.kk[:], 2, None, A.arith_shift_right))
-    after(k_m)
-    V(v.tensor_scalar(T.m80[:], T.m3[:], float(ST), None, A.mult))
-    after()
-    V(v.tensor_tensor(T.f1[:], T.m80[:], T.ks[:], A.add))
-    after()
-    V(v.tensor_tensor(T.f2[:], T.f1[:, 0:32], T.f1[:, 32:64], A.max))
-    after()
-    V(v.tensor_tensor(T.f3[:], T.f2[:, 0:16], T.f2[:, 16:32], A.max))
-    after()
-    k_fl = V(v.tensor_copy(T.flu[:], T.f3[:]))
-
-    v.wait_ge(S.p2c, arrive)
-    after()
-    s.wait_ge(S.sv, k_fl)
-    s.wait_ge(S.sa, cnt["sa"])
-    s.wait_ge(S.p2s, arrive)
     H = COLS // 2
-    mm = {}
-    for h in range(2):
-        part = slice(H * h, H * h + H)
-        te.wait_ge(S.sv, pick(v, T.finq[:, part], T.land2q[:], T.flu[:, 8 * h:8 * h + 8]))
-        te.wait_ge(S.sa, pick(s, T.fins[:, part], T.land2s[:], T.flu[:, 8 * h:8 * h + 8]))
+    halves = [(0, H, 0, 8), (H, COLS, 8, 16)]
+    for a, b, i, j in halves:
+        pick("v", ("finq", a, b), "land2q", ("flu", i, j))
+    for q, (a, b, i, j) in zip("sv", halves):
+        pick(q, ("fins", a, b), "land2s", ("flu", i, j))
+        need("t", "finq", "fins", "wq", "ws")
         for o in range(O):
-            b = 512 * (2 * h + o)
-            mm[h, o] = note(te.matmul_mx(T.ps[:, b:b + H], T.wq[:, 128 * o:128 * o + 128], T.ws[:, 128 * o:128 * o + 128],
-                                         T.finq[:, part], T.fins[:, part], True, True), "st")
-    for h in range(2):
-        b = 1024 * h
-        v.wait_ge(S.st, mm[h, 0])
-        V(v.tensor_copy(T.yb[:, H * h:H * h + H], T.ps[:, b:b + H]))
-        s.wait_ge(S.st, mm[h, 1])
-        C(s.activation(T.yb[:, COLS + H * h:COLS + H * h + H], T.ps[:, b + 512:b + 512 + H], F.Copy))
-    sy.wait_ge(S.sv, cnt["sv"])
-    sy.dma_start(T.y[:, 0:COLS], T.yb[:, 0:COLS]).then_inc(S.yo0, 16)
-    s.wait_ge(S.sa, cnt["sa"])
-    s.dma_start(T.y[:, COLS:2 * COLS], T.yb[:, COLS:2 * COLS]).then_inc(S.yo1, 16)
-    sy.wait_ge(S.yo0, 16)
-    s.wait_ge(S.yo1, 16)
-    g.wait_ge(S.sent, cnt["sent"])
-    g.wait_ge(S.sg, cnt["sg"])
+            p, wc = 512 * (a // H * O + o), (128 * o, 128 * o + 128)
+            done("t", te.matmul_mx(T.ps[:, p:p + H], ap(("wq",) + wc), ap(("ws",) + wc), ap(("finq", a, b)), ap(("fins", a, b)),
+                                   True, True), ["ps%d" % p])
+    for a, b, i, j in halves:
+        for o, q in enumerate("vs"):
+            p = 512 * (a // H * O + o)
+            need(q, "ps%d" % p)
+            y = T.yb[:, COLS * o + a:COLS * o + b]
+            done(q, v.tensor_copy(y, T.ps[:, p:p + H]) if q == "v" else s.activation(y, T.ps[:, p:p + H], F.Copy), ["yb"])
+    need("y", "yb")
+    done("y", sy.dma_start(T.y[:, :], T.yb[:, :]), ["out"], "yo", 16)
+    hold("y", "yo", cnt["yo"])
+    hold("g", "sent", cnt["sent"])
+    hold("g", "sg", cnt["sg"])

@@ -8,16 +8,17 @@ ST = 80
 LC = ST // 16
 W1, W2 = COLS + 32, N * COLS + 32
 NONE = -8192.0
+RND = 160.0
 BUFFERS = {
     "float8_e4m3fn_x4": "xq 256 wq 256 slot1q 256 land1q 256 slot2q 240 land2q 320 finq 256",
     "uint8": "xs 256 ws 256 slot1s 256 land1s 256 slot2s 240 land2s 320 fins 256",
-    "bfloat16": "xb 1024 wb 1024 restart 128 ones 128 val2 256 ind 128 indt 128 ind2 128 cr 128 crt 128 cum 128 z 128 pp 128 "
-                "pm 128 pm2 64 pm3 32 win2 1056 wt2 1056 vout 64 vland 64 cn 4 cland 32",
-    "float32": "odd 1 even 1 odd4 1 odd16 1 lowf 1 lows 1 tti 20 tt 20 pos 16 t1 16 t2 16 win1 288 wt1 288 selm 1 selb 1 selk 4 "
-               "self 4 tsf 16 cz 4 eb 21 nn 20 sf 20 xx 25 dd 20 h1 60 h2 30 h3 15 g1 20 g2 10 g3 5 s4 20 cf 20 f1 64 f2 32 f3 16 "
-               "yb 512",
-    "int32": "part 1 par 1 low 1 bit 1 val1 256 ew 32 ec 32 si 16 cb 30 aa 20 pb 30 vi 64 m3 64 m80 64 kk 64 ks 64",
-    "uint16": "off1 16 l1u 16 off2 16 l2u 16 lou 6 flu 16 sel 4 selr 4",
+    "bfloat16": "xb 1024 wb 1024 zb 288 restart 64 low0 64 val2 256 ec 32 ind 64 indt 64 cr 64 crt 64 cum 64 z 64 pp 64 pm 64 pm2 32 "
+                "bc 64 bt 64 win2 1056 wt2 1056 vout 64 vland 64 cn 4 cland 32 aa 20",
+    "float32": "odd 1 odd4 1 odd16 1 start 1 q0 1 q1 1 lowf 1 lows 1 tti 20 tt 20 ttl 5 pos 16 t1 16 t2 16 win1 288 wt1 288 selm 1 "
+               "selb 1 selk 4 self 4 eb 21 lo 20 hi 20 sf 20 xx 20 dd 20 h1 60 h2 30 h3 15 g1 20 g2 10 g3 5 s4 20 cf 20 "
+               "f1 64 f2 32 f3 16 yb0 256 yb1 256",
+    "int32": "part 1 par 1 low 1 bit 1 val1 256 ew 16 si 16 cb 30 pb 30 vi 64 m3 64 m80 64 kk 64 ks 64",
+    "uint16": "off1 16 l1u 16 off2 16 l2u 16 lou 6 flu 16 sel 4 selr 4 selz 4",
 }
 SCRATCH = {"ps": ("psum", [128, 2048], "float32")}
 for _t, _l in BUFFERS.items():
@@ -78,6 +79,9 @@ def rank_program(g, core, T, topo):
     def named(*xs):
         return [name(x) for x in xs if isinstance(x, (str, tuple))]
 
+    def val(x):
+        return ap(x) if isinstance(x, (str, tuple)) else x
+
     def done(q, ins, out, sem=None, by=1):
         sem = sem or own_sem[q]
         ins.then_inc(S[sem], by)
@@ -95,16 +99,16 @@ def rank_program(g, core, T, topo):
 
     def ts(out, a, s1, op, s2=None, op2=None):
         need("v", *named(a, s1, s2))
-        s1, s2 = [ap(k) if isinstance(k, (str, tuple)) else k for k in (s1, s2)]
-        done("v", v.tensor_scalar(ap(out), ap(a), s1, s2, op, op2) if op2 else v.tensor_scalar(ap(out), ap(a), s1, None, op), [out])
+        a, s1, s2 = ap(a), val(s1), val(s2)
+        done("v", v.tensor_scalar(ap(out), a, s1, s2, op, op2) if op2 else v.tensor_scalar(ap(out), a, s1, None, op), [out])
 
     def tr(out, i):
         need("v", i)
         done("v", v.transpose(ap(out), ap(i)), [out])
 
-    def scan(out, a, b, op):
-        need("v", a, b)
-        done("v", v.tensor_tensor_scan(ap(out), ap(a), ap(b), 0.0, A.mult, op), [out])
+    def scan(out, a, b, initial, op0, op1):
+        need("v", *named(a, b, initial))
+        done("v", v.tensor_tensor_scan(ap(out), ap(a), ap(b), val(initial), op0, op1), [out])
 
     def fill(x, c):
         done("v", v.memset(ap(x), c), [x])
@@ -115,7 +119,7 @@ def rank_program(g, core, T, topo):
 
     def act(out, i, offs=None, **kw):
         need("s", *named(i, offs, *kw.values()))
-        kw = {k: ap(x) if isinstance(x, (str, tuple)) else x for k, x in kw.items()}
+        kw = {k: val(x) for k, x in kw.items()}
         done("s", s.activation(ap(out), ap(i) if offs is None else ap(i).indirect(ap(offs)), F.Identity, **kw), [out])
 
     def load(q, out, src, sem):
@@ -146,79 +150,84 @@ def rank_program(g, core, T, topo):
         cnt["sent"] += leave
         made.setdefault(name(dst), {})[sem] = arrive
 
-    fill("ew", -1)
-    k_ew = cnt["sv"]
+    for q, k0 in (("y", 0), ("s", 4)):
+        for k in range(k0, k0 + 4):
+            done(q, queue[q].dma_start(T.ew[16 * k:16 * k + 16, :], T.to[:, :]), ["ew"], "ld_e", 16)
+    load("y", "xb", T.x[:, :], "ld_x")
+    fill("zb", 0.0)
     iota("part", [[1, 1]], 0, 1, True)
     iota("val1", [[1, 16], [16, 16]], 0, 0, True)
     k_val = cnt["sg"]
-    for q, k0 in (("y", 0), ("s", 2)):
-        hold(q, "sv", k_ew)
-        for k in (k0, k0 + 1):
-            for a in (0, 16):
-                done(q, queue[q].dma_start(T.ew[32 * k + a:32 * k + a + 16, a:a + 16], T.to[:, :]), ["ew"], "ld_e", 16)
     for q, k0 in (("y", 0), ("s", 4)):
         hold(q, "sg", k_val)
         for k in range(k0, k0 + 4):
             done(q, queue[q].dma_start(T.val1[16 * k + 1:16 * k + 2, :], T.to[:, :]), ["val1"], "ld_r", 16)
-    load("y", "xb", T.x[:, :], "ld_x")
     load("y", "wb", T.w[:, :], "ld_w")
 
-    fill("win1", 0.0)
-    act("restart", ("win1", 0, 128), bias=1.0)
-    act("ones", ("win1", 0, 128), bias=1.0)
-    need("s", "restart")
-    act(("restart", 0, 128, 16), ("win1", 0, 8))
-    for a in range(0, W2, W1):
-        n = min(W1, W2 - a)
-        act(("win2", a, a + n), ("win1", 0, n), bias=NONE)
-    act("eb", ("win1", 0, 21))
-    act(("cn", 3, 4), ("win1", 0, 1), bias=float(COLS))
-    act(("xx", 0, 5), ("win1", 0, 5))
-    need("s", "eb")
-    act(("eb", 4, 20, 5), ("win1", 0, 4), bias=float(COLS))
-    k_zero = cnt["sa"]
     iota("selk", [[16 * 16, 4]])
     iota("tti", [[-PK1, N], [16, LC]])
     iota(("cb", 0, 10), [[0, 10]], 0, 0, True)
     iota(("pb", 0, 10), [[0, 10]], 0, 0, True)
     iota("val2", [[1, N], [N, PK1]])
     ts("par", "part", 4, A.logical_shift_right, 1, A.bitwise_and)
-    ts("low", "part", 15, A.bitwise_and)
-    ts("bit", "part", 1, A.bitwise_and)
     cp("odd", "par")
-    ts("even", "par", -1.0, A.mult, 1.0, A.add)
+    ts("q0", "odd", 3.0, A.mult, RND, A.add)
+    ts("q1", "odd", RND + 1.0, A.add)
+    ts("start", "odd", -(COLS - 1.0), A.mult)
     ts("odd4", "par", 0.25, A.mult)
     ts("odd16", "par", 16.0, A.mult)
+    ts("low", "part", 15, A.bitwise_and)
+    ts("bit", "part", 1, A.bitwise_and)
     ts("selm", "par", -64.0, A.mult, 32.0, A.add)
     cp("lowf", "low")
     ts("selb", "bit", ("selm", 0, 1), A.mult, ("odd16", 0, 1), A.add)
-    ts("tt", "tti", ("lowf", 0, 1), A.add)
     ts("lows", "low", 16.0, A.mult, ("selb", 0, 1), A.add)
+    ts("selz", "selk", 1.0 / 16, A.mult, 15.0, A.add)
     ts("self", "selk", ("lows", 0, 1), A.add)
     cp("sel", "self")
     ts("selr", "self", 1.0, A.add)
+    ts("tt", "tti", ("lowf", 0, 1), A.add)
+    act("restart", ("zb", 0, 64), bias=1.0)
+    act("low0", ("zb", 0, 64), bias=-NONE)
+    need("s", "restart", "low0")
+    act(("restart", 0, 64, 16), ("zb", 0, 4))
+    act(("low0", 16, 17), ("zb", 0, 1), bias=("start", 0, 1))
+    act("eb", ("zb", 0, 21))
+    act(("cn", 3, 4), ("zb", 0, 1), bias=float(COLS))
+    need("s", "eb")
+    act(("eb", 4, 20, 5), ("zb", 0, 4), bias=float(COLS))
+    act("win1", "zb")
 
-    ts("ec", "ew", 8, A.arith_shift_right)
-    for q in range(N):
-        ts(("ind", 32 * q, 32 * q + 32), "ec", float(q), A.is_equal)
+    for a in (0, 16):
+        ts(("ec", a, a + 16), "ew", 1.0 / COLS, A.mult, RND - 0.498, A.add)
+    for u in (0, 1):
+        ts(("ind", 32 * u, 32 * u + 32), "ec", ("q%d" % u, 0, 1), A.is_equal)
     tr("indt", "ind")
-    scan("cr", "restart", "indt", A.add)
-    cp("ind2", "indt")
+    scan("cr", "restart", "indt", 0.0, A.mult, A.add)
     tr("crt", "cr")
-    scan("cum", "ones", "crt", A.add)
+    scan(("cum", 0, 48), ("low0", 0, 48), ("crt", 0, 48), ("start", 0, 1), A.min, A.add)
+    scan(("cum", 48, 64), ("low0", 48, 64), ("crt", 48, 64), ("cum", 31, 32), A.min, A.add)
     tr("z", "cum")
-    tt(("ind2", 0, 128, 16), ("indt", 0, 128, 16), ("z", 15, 128, 16), A.subtract)
-    scan("pp", "restart", "ind2", A.subtract)
+    need("v", "z", "selz", "cr")
+    done("v", v.tensor_tensor(ap("pp"), ap("z").indirect(ap("selz")), ap("cr"), A.subtract), ["pp"])
     tt("pm", "pp", "indt", A.mult)
-    tt("pm2", ("pm", 0, 64), ("pm", 64, 128), A.add)
-    tt("pm3", ("pm2", 0, 32), ("pm2", 32, 64), A.add)
-    tt("pos", ("pm3", 0, 16), ("pm3", 16, 32), A.add)
+    for i, c in enumerate((31, 47)):
+        act(("bc", 32 * i, 32 * i + 32), ("zb", 0, 32), bias=("cum", c, c + 1))
+    tr("bt", "bc")
+    tt("pm2", ("pm", 0, 32), ("pm", 32, 64), A.add)
+    tt("pos", ("pm2", 0, 16), ("pm2", 16, 32), A.subtract)
     ts("si", "pos", 0.25, A.mult, -0.375, A.add)
     ts("t1", "si", -(4.0 * PK1 - 1) / PK1, A.mult, ("odd4", 0, 1), A.add)
     tt("t2", "pos", "t1", A.add)
     ts("off1", "t2", float(PK1), A.mult)
+
+    act(("cn", 0, 3), ("bt", 15, 48, 16))
+    cp(("cland", 8 * me, 8 * me + 4), "cn", "s")
+    for a in range(0, W2, W1):
+        n = min(W1, W2 - a)
+        act(("win2", a, a + n), ("zb", 0, n), bias=NONE)
+
     need("v", "val1", "off1", "win1")
-    hold("v", "sa", k_zero)
     done("v", v.tensor_copy(T.win1[:, 0:W1].indirect(T.off1[:, 0:16]), T.val1[:, 0:COLS]), ["win1"])
     tr("wt1", "win1")
     quant("x")
@@ -228,15 +237,7 @@ def rank_program(g, core, T, topo):
     a1, b1 = PK1 * me, PK1 * (me + 1)
     for a, b in runs:
         pick("v", ("slot1q", a, b), "xq", ("l1u", a // 16, b // 16))
-    pick("v", ("land1q", a1, b1), "xq", ("l1u", a1 // 16, b1 // 16))
-
-    act("cz", ("z", 31, 128, 32), scale=("even", 0, 1))
-    for q in range(N - 1):
-        act(("cn", q, q + 1), ("z", 32 * q + 15, 32 * q + 16), bias=("cz", q + 1, q + 2), scale=("odd", 0, 1))
-    cp(("cland", 8 * me, 8 * me + 4), "cn", "s")
-    for a, b in runs:
         pick("s", ("slot1s", a, b), "xs", ("l1u", a // 16, b // 16))
-    act("tsf", "wt1", ("selr", 0, 1), bias=("odd16", 0, 1))
     pick("s", ("land1s", a1, b1), "xs", ("l1u", a1 // 16, b1 // 16))
 
     send("cnt", "cn", ("cland", 8 * me, 8 * me + 4), lambda d: (0, 4))
@@ -244,32 +245,35 @@ def rank_program(g, core, T, topo):
     send("p1c", "slot1q", ("land1q", a1, b1), cut1, True)
     send("p1s", "slot1s", ("land1s", a1, b1), cut1)
 
-    cp("off2", "tsf")
+    need("v", "wt1", "selr", "odd16")
+    done("v", v.tensor_scalar(T.off2[:], T.wt1[:, 0:W1].indirect(T.selr[:, 0:1]), T.odd16[:, 0:1], None, A.add), ["off2"])
     need("v", "val2", "off2", "win2")
     done("v", v.tensor_copy(T.win2[:, 0:W2].indirect(T.off2[:, 0:16]), T.val2[:, 0:COLS]), ["win2"])
     tr("wt2", "win2")
-    for q in range(N - 1):
-        cp(("eb", q + 1, 20, 5), ("cland", q, 32, 8), "s")
+    pick("v", ("land1q", a1, b1), "xq", ("l1u", a1 // 16, b1 // 16))
+    act("ttl", ("tt", 0, LC), bias=-RND)
+    for i, q, kw in ((0, 1, {}), (2, 2, {}), (1, 3, {"scale": -1.0, "bias": 1.0})):
+        act(("eb", q, 20, 5), ("cland", i, 32, 8), **kw)
+    act("lo", ("eb", 0, 20), scale=0.25)
+    act("hi", ("eb", 1, 21), scale=0.25, bias=0.375 - PK1)
+    act("aa", ("eb", 0, 20), scale=0.25, bias=RND + (N - 1 - me) / 4.0 - 0.375)
     act("vout", "wt2", "sel")
     send("plc", "vout", ("vland", 16 * me, 16 * me + 16), lambda d: (16 * d, 16 * d + 16))
 
-    tt("nn", ("eb", 1, 21), ("eb", 0, 20), A.subtract)
-    ts("aa", ("eb", 0, 20), 0.25, A.mult, (N - 1 - me) / 4.0 - 0.375, A.add)
-    ts(("cb", 10, 30), "nn", 0.25, A.mult, 0.375 - PK1, A.add)
+    tt(("cb", 10, 30), "hi", "lo", A.subtract)
     tt(("pb", 10, 30), ("cb", 5, 25), ("cb", 0, 20), A.add)
     tt("sf", ("pb", 10, 30), ("pb", 0, 20), A.add)
-    tt(("xx", 5, 25), "aa", "sf", A.subtract)
-    tt("dd", ("xx", 5, 25), ("xx", 0, 20), A.subtract)
+    tt("xx", "aa", "sf", A.subtract)
+    tt(("dd", 5, 20), ("xx", 5, 20), ("xx", 0, 15), A.subtract)
 
     def steps(dests, b1, b2, b3, lst):
         n = LC * len(dests)
-        for r in range(N):
+        for x, d in enumerate(dests):
+            act((b1, LC * x, LC * x + LC), "ttl", bias=("aa", d, d + 1))
+        for r in range(1, N):
             for x, d in enumerate(dests):
                 o, i = (b1, n * r + LC * x, n * r + LC * x + LC), 5 * r + d
-                if r == 0:
-                    ts(o, ("tt", 0, LC), ("dd", i, i + 1), A.add)
-                else:
-                    ts(o, ("tt", LC * r, LC * r + LC), ("sf", i, i + 1), A.is_ge, ("dd", i, i + 1), A.mult)
+                ts(o, ("tt", LC * r, LC * r + LC), ("sf", i, i + 1), A.is_ge, ("dd", i, i + 1), A.mult)
         tt(b2, (b1, 0, 2 * n), (b1, 2 * n, 4 * n), A.add)
         tt(b3, (b2, 0, n), (b2, n, 2 * n), A.add)
         ts((lst, 0, n), b3, float(COLS - 1), A.min)
@@ -282,13 +286,13 @@ def rank_program(g, core, T, topo):
     pick("v", ("land2q",) + own2, "land1q", ("lou", 0, LC))
     pick("s", "slot2s", "land1s", ("l2u", 0, 3 * LC))
     cp(("vland", 16 * me, 16 * me + 16), ("vout", 16 * me, 16 * me + 16), "s")
+    act("s4", "sf", scale=4.0)
     pick("s", ("land2s",) + own2, "land1s", ("lou", 0, LC))
     cut2 = lambda d: (ST * others.index(d), ST * others.index(d) + PK2)
     send("p2c", "slot2q", ("land2q",) + pk2, cut2, True)
     send("p2s", "slot2s", ("land2s",) + pk2, cut2)
 
     quant("w")
-    ts("s4", "sf", 4.0, A.mult)
     tt("cf", "s4", ("eb", 0, 20), A.subtract)
     cp("vi", "vland")
     for r in range(N):
@@ -308,19 +312,20 @@ def rank_program(g, core, T, topo):
         pick("v", ("finq", a, b), "land2q", ("flu", i, j))
     for q, (a, b, i, j) in zip("sv", halves):
         pick(q, ("fins", a, b), "land2s", ("flu", i, j))
-        need("t", "finq", "fins", "wq", "ws")
-        for o in range(O):
-            p, wc = 512 * (a // H * O + o), (128 * o, 128 * o + 128)
+    need("t", "finq", "fins", "wq", "ws")
+    for o in range(O):
+        for h, (a, b, i, j) in enumerate(halves):
+            p, wc = 512 * (2 * o + h), (128 * o, 128 * o + 128)
             done("t", te.matmul_mx(T.ps[:, p:p + H], ap(("wq",) + wc), ap(("ws",) + wc), ap(("finq", a, b)), ap(("fins", a, b)),
                                    True, True), ["ps%d" % p])
-    for a, b, i, j in halves:
-        for o, q in enumerate("vs"):
-            p = 512 * (a // H * O + o)
+    for o in range(O):
+        for h, q in enumerate("vs"):
+            p, y = 512 * (2 * o + h), ("yb%d" % o, H * h, H * h + H)
             need(q, "ps%d" % p)
-            y = T.yb[:, COLS * o + a:COLS * o + b]
-            done(q, v.tensor_copy(y, T.ps[:, p:p + H]) if q == "v" else s.activation(y, T.ps[:, p:p + H], F.Copy), ["yb"])
-    need("y", "yb")
-    done("y", sy.dma_start(T.y[:, :], T.yb[:, :]), ["out"], "yo", 16)
+            done(q, v.tensor_copy(ap(y), T.ps[:, p:p + H]) if q == "v" else s.activation(ap(y), T.ps[:, p:p + H], F.Copy), [y])
+    for o, q in enumerate("ys"):
+        need(q, "yb%d" % o)
+        done(q, queue[q].dma_start(T.y[:, COLS * o:COLS * o + COLS], T["yb%d" % o][:]), ["out"], "yo", 16)
     hold("y", "yo", cnt["yo"])
     hold("g", "sent", cnt["sent"])
     hold("g", "sg", cnt["sg"])

@@ -2,30 +2,33 @@ from concourse.bass import DstId, RemoteDMATransfer
 from concourse.mybir import dt, AluOpType, ActivationFunctionType
 
 N, COLS, O = 4, 256, 2
+H = COLS // 2
 PK1 = COLS // N
 PK2 = COLS // N + N - 1
 ST = 80
 LC = ST // 16
-W1, W2 = COLS + 32, N * COLS + 32
+W1 = N * ST
+W2 = N * COLS
 NONE = -8192.0
 RND = 160.0
+MID = 128.0
 BUFFERS = {
-    "float8_e4m3fn_x4": "xq 256 wq 256 slot1q 256 land1q 256 slot2q 240 land2q 320 finq 256",
-    "uint8": "xs 256 ws 256 slot1s 256 land1s 256 slot2s 240 land2s 320 fins 256",
-    "bfloat16": "xb 1024 wb 1024 zb 288 restart 64 low0 64 val2 256 ec 32 ind 64 indt 64 cr 64 crt 64 cum 64 z 64 pp 64 pm 64 pm2 32 "
-                "bc 64 bt 64 win2 1056 wt2 1056 vout 64 vland 64 cn 4 cland 32 aa 20",
-    "float32": "odd 1 odd4 1 odd16 1 start 1 q0 1 q1 1 lowf 1 lows 1 tti 20 tt 20 ttl 5 pos 16 t1 16 t2 16 win1 288 wt1 288 selm 1 "
-               "selb 1 selk 4 self 4 eb 21 lo 20 hi 20 sf 20 xx 20 dd 20 h1 60 h2 30 h3 15 g1 20 g2 10 g3 5 s4 20 cf 20 "
-               "f1 64 f2 32 f3 16 yb0 256 yb1 256",
-    "int32": "part 1 par 1 low 1 bit 1 val1 256 ew 16 si 16 cb 30 pb 30 vi 64 m3 64 m80 64 kk 64 ks 64",
-    "uint16": "off1 16 l1u 16 off2 16 l2u 16 lou 6 flu 16 sel 4 selr 4 selz 4",
+    "float8_e4m3fn_x4": "xq 256 wq 256 slot1q 192 land1q 256 slot2q 240 land2q 320 finq0 128 finq1 128",
+    "uint8": "xs 256 ws 256 slot1s 192 land1s 256 slot2s 240 land2s 320 fins0 128 fins1 128",
+    "bfloat16": "xb 1024 wb 1024 zb 64 restart 64 low0 64 val1 256 ec 32 ind 64 indt 64 cr 64 crt 64 cum 64 z 64 pp 64 pm 64 pm2 32 "
+                "bc 64 bt 64 win1 320 wt1 320 vt 16 prow 128 win2 1024 vo 64 vland 64 cn 4 cland 32 aa 20 aq 20 bu 4 bv 4",
+    "float32": "odd 1 odd5 1 odd8 1 bth 1 bcc 1 start 1 q0 1 q1 1 lowf 1 selm 1 sela 1 selb 1 tti 5 ttl 5 twi 80 ttw 80 cji 4 cj 4 "
+               "bv4 4 bd 4 bg 4 be 4 bs 4 r64 4 r64b 4 pos 16 t1 16 t2 16 eb 21 lo 20 hi 20 sf 20 xx 20 dd 20 ge 64 h1 84 h2 40 h3 20 "
+               "e80 4 q320 4 th 4 xa 4 cc 4 kk 64 f1 64 f2 32 f3 32 f3t 32 f4 16 yb0 256 yb1 256",
+    "int32": "part 1 par 1 low 1 mq 1 gm 1 la 1 lb 1 bit 1 ew 16 si 16 cb 30 pb 30 selk 4",
+    "uint16": "off1 16 l1u 16 eu 16 l2u 20 lou 6 flu 16 sel 2 selh 2 selz 4 bl 4",
 }
 SCRATCH = {"ps": ("psum", [128, 2048], "float32")}
 for _t, _l in BUFFERS.items():
     _w = _l.split()
     for _n, _c in zip(_w[0::2], _w[1::2]):
         SCRATCH[_n] = ("sbuf", [128, int(_c)], _t)
-SEMAPHORES = "sv sa sg st ld_e ld_x ld_r ld_w cnt p1c p1s plc p2c p2s sent yo".split()
+SEMAPHORES = "sv sa sg st ld_e ld_x ld_w vf vr vo vw cnt p1c p1s plc p2c p2s sent yo".split()
 
 
 def plan(src, cores, topo):
@@ -49,7 +52,8 @@ def rank_program(g, core, T, topo):
         return
     A, F = AluOpType, ActivationFunctionType
     S = T.sem
-    others = [d for d in range(N) if d != me]
+    turn = [(me + 1 + i) % N for i in range(N)]
+    others = turn[:N - 1]
     mine = plan(core, T.cores, topo)
     arrive = sum(len(plan(T.cores[r], T.cores, topo)[core]) for r in others)
     leave = sum(len(e) for e in mine.values())
@@ -93,9 +97,10 @@ def rank_program(g, core, T, topo):
         need(q, name(i))
         done(q, v.tensor_copy(ap(out), ap(i)) if q == "v" else s.activation(ap(out), ap(i), F.Copy), [out])
 
-    def tt(out, a, b, op):
-        need("v", name(a), name(b))
-        done("v", v.tensor_tensor(ap(out), ap(a), ap(b), op), [out])
+    def tt(out, a, b, op, offs=None):
+        need("v", *named(a, b, offs))
+        a = ap(a) if offs is None else ap(a).indirect(ap(offs))
+        done("v", v.tensor_tensor(ap(out), a, ap(b), op), [out])
 
     def ts(out, a, s1, op, s2=None, op2=None):
         need("v", *named(a, s1, s2))
@@ -117,21 +122,20 @@ def rank_program(g, core, T, topo):
         kw = {} if whole else {"allow_small_or_imprecise_dtypes": True}
         done("g", g.iota(ap(out), pat, base, cm, **kw), [out])
 
-    def act(out, i, offs=None, **kw):
-        need("s", *named(i, offs, *kw.values()))
-        kw = {k: val(x) for k, x in kw.items()}
-        done("s", s.activation(ap(out), ap(i) if offs is None else ap(i).indirect(ap(offs)), F.Identity, **kw), [out])
+    def act(out, i, **kw):
+        need("s", *named(i, *kw.values()))
+        done("s", s.activation(ap(out), ap(i), F.Identity, **{k: val(x) for k, x in kw.items()}), [out])
 
     def load(q, out, src, sem):
         done(q, queue[q].dma_start(ap(out), src), [out], sem, 16)
 
-    def quant(k):
+    def quant(k, a, b):
         need("v", k + "b")
-        done("v", v.quantize_mx(ap(k + "q"), ap(k + "s"), ap(k + "b")), [k + "q", k + "s"])
+        done("v", v.quantize_mx(ap((k + "q", a, b)), ap((k + "s", a, b)), ap((k + "b", 4 * a, 4 * b))), [k + "q", k + "s"])
 
     def pick(q, out, win, offs):
         need(q, win, name(offs))
-        if name(out)[-1] == "q":
+        if win[-1] == "q":
             done(q, v.tensor_copy(ap(out).bitcast(dt.uint32), ap(win).bitcast(dt.uint32).indirect(ap(offs))), [out])
         elif q == "v":
             done(q, v.tensor_copy(ap(out), ap(win).indirect(ap(offs))), [out])
@@ -154,49 +158,56 @@ def rank_program(g, core, T, topo):
         for k in range(k0, k0 + 4):
             done(q, queue[q].dma_start(T.ew[16 * k:16 * k + 16, :], T.to[:, :]), ["ew"], "ld_e", 16)
     load("y", "xb", T.x[:, :], "ld_x")
-    fill("zb", 0.0)
-    iota("part", [[1, 1]], 0, 1, True)
-    iota("val1", [[1, 16], [16, 16]], 0, 0, True)
-    k_val = cnt["sg"]
-    for q, k0 in (("y", 0), ("s", 4)):
-        hold(q, "sg", k_val)
-        for k in range(k0, k0 + 4):
-            done(q, queue[q].dma_start(T.val1[16 * k + 1:16 * k + 2, :], T.to[:, :]), ["val1"], "ld_r", 16)
     load("y", "wb", T.w[:, :], "ld_w")
+    fill("zb", 0.0)
+    fill(("win2", 0, COLS), NONE)
+    need("y", "win2")
+    for a in range(COLS, W2, COLS):
+        done("y", sy.dma_start(T.win2[:, a:a + COLS], T.win2[:, 0:COLS]), ["blank"], "vf", 16)
 
-    iota("selk", [[16 * 16, 4]])
-    iota("tti", [[-PK1, N], [16, LC]])
+    iota("part", [[1, 1]], 0, 1, True)
+    iota("selk", [[16, 4]], 15, 0, True)
+    iota("val1", [[1, 16], [16, 16]])
+    iota("cji", [[16, 4]])
+    iota("twi", [[-PK1, 4], [0, N], [16, LC]], -PK1)
+    iota("tti", [[16, LC]], -int(RND))
     iota(("cb", 0, 10), [[0, 10]], 0, 0, True)
     iota(("pb", 0, 10), [[0, 10]], 0, 0, True)
-    iota("val2", [[1, N], [N, PK1]])
+    iota("r64", [[PK1, N]], int(RND + MID) - 1)
     ts("par", "part", 4, A.logical_shift_right, 1, A.bitwise_and)
+    ts("low", "part", 15, A.bitwise_and)
+    ts("mq", "part", 2, A.logical_shift_right, 3, A.bitwise_and)
     cp("odd", "par")
+    cp("lowf", "low")
+    tt("la", "low", "mq", A.add)
+    ts("gm", "low", 4 * (N - 1 - me) - 0.5, A.is_ge, -float(N * LC), A.mult)
     ts("q0", "odd", 3.0, A.mult, RND, A.add)
     ts("q1", "odd", RND + 1.0, A.add)
-    ts("start", "odd", -(COLS - 1.0), A.mult)
-    ts("odd4", "par", 0.25, A.mult)
-    ts("odd16", "par", 16.0, A.mult)
-    ts("low", "part", 15, A.bitwise_and)
-    ts("bit", "part", 1, A.bitwise_and)
-    ts("selm", "par", -64.0, A.mult, 32.0, A.add)
-    cp("lowf", "low")
-    ts("selb", "bit", ("selm", 0, 1), A.mult, ("odd16", 0, 1), A.add)
-    ts("lows", "low", 16.0, A.mult, ("selb", 0, 1), A.add)
-    ts("selz", "selk", 1.0 / 16, A.mult, 15.0, A.add)
-    ts("self", "selk", ("lows", 0, 1), A.add)
-    cp("sel", "self")
-    ts("selr", "self", 1.0, A.add)
-    ts("tt", "tti", ("lowf", 0, 1), A.add)
+    tt("lb", "la", "gm", A.add)
+    ts("bit", "lb", 1, A.bitwise_and)
+    flip = LC * (me + 1) % 2
+    act("sela", "odd", scale=16.0 - 64.0 * flip, bias=16.0 * LC * (me + 1) + 32.0 * flip)
+    act("selm", "odd", scale=-64.0 * (1 - 2 * flip), bias=32.0 * (1 - 2 * flip))
+    act("odd8", "odd", scale=8.0)
+    act("start", "odd", scale=-(COLS - 1.0))
     act("restart", ("zb", 0, 64), bias=1.0)
     act("low0", ("zb", 0, 64), bias=-NONE)
+    act("odd5", "odd", scale=1.0 / LC)
     need("s", "restart", "low0")
     act(("restart", 0, 64, 16), ("zb", 0, 4))
     act(("low0", 16, 17), ("zb", 0, 1), bias=("start", 0, 1))
     act("eb", ("zb", 0, 21))
+    act(("dd", 0, 5), ("zb", 0, 5))
     act(("cn", 3, 4), ("zb", 0, 1), bias=float(COLS))
     need("s", "eb")
     act(("eb", 4, 20, 5), ("zb", 0, 4), bias=float(COLS))
-    act("win1", "zb")
+    act(("win1", 0, COLS), "val1", scale=0.0)
+    act(("win1", COLS, W1), ("zb", 0, W1 - COLS))
+    act("prow", ("val1", 0, H), scale=0.0)
+    ts("selb", "bit", ("selm", 0, 1), A.mult, ("sela", 0, 1), A.add)
+    cp("selz", "selk")
+    ts(("sel", 0, 1), "lb", 16.0, A.mult, ("selb", 0, 1), A.add)
+    ts(("selh", 0, 1), "low", ("odd8", 0, 1), A.add, 15.0, A.min)
 
     for a in (0, 16):
         ts(("ec", a, a + 16), "ew", 1.0 / COLS, A.mult, RND - 0.498, A.add)
@@ -208,118 +219,128 @@ def rank_program(g, core, T, topo):
     scan(("cum", 0, 48), ("low0", 0, 48), ("crt", 0, 48), ("start", 0, 1), A.min, A.add)
     scan(("cum", 48, 64), ("low0", 48, 64), ("crt", 48, 64), ("cum", 31, 32), A.min, A.add)
     tr("z", "cum")
-    need("v", "z", "selz", "cr")
-    done("v", v.tensor_tensor(ap("pp"), ap("z").indirect(ap("selz")), ap("cr"), A.subtract), ["pp"])
-    tt("pm", "pp", "indt", A.mult)
+    tt("pp", "z", "cr", A.subtract, "selz")
     for i, c in enumerate((31, 47)):
         act(("bc", 32 * i, 32 * i + 32), ("zb", 0, 32), bias=("cum", c, c + 1))
+    tt("pm", "pp", "indt", A.mult)
     tr("bt", "bc")
     tt("pm2", ("pm", 0, 32), ("pm", 32, 64), A.add)
     tt("pos", ("pm2", 0, 16), ("pm2", 16, 32), A.subtract)
     ts("si", "pos", 0.25, A.mult, -0.375, A.add)
-    ts("t1", "si", -(4.0 * PK1 - 1) / PK1, A.mult, ("odd4", 0, 1), A.add)
+    ts("t1", "si", -(4.0 * ST - 1) / ST, A.mult, ("odd5", 0, 1), A.add)
     tt("t2", "pos", "t1", A.add)
-    ts("off1", "t2", float(PK1), A.mult)
+    ts("off1", "t2", float(ST), A.mult)
 
     act(("cn", 0, 3), ("bt", 15, 48, 16))
     cp(("cland", 8 * me, 8 * me + 4), "cn", "s")
-    for a in range(0, W2, W1):
-        n = min(W1, W2 - a)
-        act(("win2", a, a + n), ("zb", 0, n), bias=NONE)
+    act("vt", "t2", scale=float(ST), bias=-MID)
+    for q, a, r in (("y", 0, 0), ("s", 24, 16)):
+        need(q, "vt", "prow")
+        for p in range(0, 128, 32):
+            done(q, queue[q].dma_start(T.prow[p + r:p + r + 1, :], T.vt[p + a:p + a + 8, :]), ["rows"], "vr", 16)
+    act("cj", "cji", bias="lowf")
+    act("ttl", "tti", bias="lowf")
+    act("ttw", "twi", bias="lowf")
+    act("bu", "cj", scale=0.2, bias=RND - 0.4)
+    act("bv", "cj", scale=0.05, bias=RND - 0.475)
+    act("bth", "odd", scale=16.0, bias=-MID - 0.5)
+    act("bcc", "odd", scale=-16.0)
+    act("bv4", "bv", scale=-4.0, bias=4 * RND)
 
     need("v", "val1", "off1", "win1")
     done("v", v.tensor_copy(T.win1[:, 0:W1].indirect(T.off1[:, 0:16]), T.val1[:, 0:COLS]), ["win1"])
+    quant("x", 0, H)
     tr("wt1", "win1")
-    quant("x")
+    quant("x", H, COLS)
     need("v", "wt1", "sel")
     done("v", v.tensor_copy(T.l1u[:], T.wt1[:, 0:W1].indirect(T.sel[:, 0:1])), ["l1u"])
-    runs = [(a, b) for a, b in ((0, PK1 * me), (PK1 * (me + 1), COLS)) if a < b]
     a1, b1 = PK1 * me, PK1 * (me + 1)
-    for a, b in runs:
-        pick("v", ("slot1q", a, b), "xq", ("l1u", a // 16, b // 16))
-        pick("s", ("slot1s", a, b), "xs", ("l1u", a // 16, b // 16))
-    pick("s", ("land1s", a1, b1), "xs", ("l1u", a1 // 16, b1 // 16))
+    mix, own = ("l1u", 0, 12), ("l1u", 12, 16)
+    pick("v", "slot1q", "xq", mix)
+    pick("s", "slot1s", "xs", mix)
+    pick("s", ("land1s", a1, b1), "xs", own)
 
     send("cnt", "cn", ("cland", 8 * me, 8 * me + 4), lambda d: (0, 4))
-    cut1 = lambda d: (PK1 * d, PK1 * (d + 1))
+    cut1 = lambda d: (PK1 * others.index(d), PK1 * (others.index(d) + 1))
     send("p1c", "slot1q", ("land1q", a1, b1), cut1, True)
     send("p1s", "slot1s", ("land1s", a1, b1), cut1)
 
-    need("v", "wt1", "selr", "odd16")
-    done("v", v.tensor_scalar(T.off2[:], T.wt1[:, 0:W1].indirect(T.selr[:, 0:1]), T.odd16[:, 0:1], None, A.add), ["off2"])
-    need("v", "val2", "off2", "win2")
-    done("v", v.tensor_copy(T.win2[:, 0:W2].indirect(T.off2[:, 0:16]), T.val2[:, 0:COLS]), ["win2"])
-    tr("wt2", "win2")
-    pick("v", ("land1q", a1, b1), "xq", ("l1u", a1 // 16, b1 // 16))
-    act("ttl", ("tt", 0, LC), bias=-RND)
+    need("v", "ew", "selh")
+    done("v", v.tensor_copy(T.eu[:], T.ew[:, 0:16].indirect(T.selh[:, 0:1])), ["eu"])
+    need("v", "rows", "prow", "eu", "win2", "blank")
+    done("v", v.tensor_copy(T.win2[:, 0:W2].indirect(T.eu[:, 0:8]), T.prow[:, 0:H]), ["win2"])
+    need("y", "win2")
+    for d in turn:
+        out = ("vo", 16 * d, 16 * d + 16) if d != me else ("vland", 16 * d, 16 * d + 16)
+        done("y", sy.dma_start(ap(out), T.win2[0:128:16, COLS * d:COLS * d + COLS]), [out], "vo" if d != me else "vw", 16)
+    send("plc", "vo", ("vland", 16 * me, 16 * me + 16), lambda d: (16 * d, 16 * d + 16))
+
     for i, q, kw in ((0, 1, {}), (2, 2, {}), (1, 3, {"scale": -1.0, "bias": 1.0})):
         act(("eb", q, 20, 5), ("cland", i, 32, 8), **kw)
     act("lo", ("eb", 0, 20), scale=0.25)
     act("hi", ("eb", 1, 21), scale=0.25, bias=0.375 - PK1)
     act("aa", ("eb", 0, 20), scale=0.25, bias=RND + (N - 1 - me) / 4.0 - 0.375)
-    act("vout", "wt2", "sel")
-    send("plc", "vout", ("vland", 16 * me, 16 * me + 16), lambda d: (16 * d, 16 * d + 16))
+    for x, d in enumerate(turn):
+        act(("h1", LC * x, LC * x + LC), "ttl", bias=("aa", d, d + 1))
+    act("aq", ("eb", 0, 20), scale=0.25, bias=RND - 0.375)
+    act("e80", ("eb", me, 20, 5), scale=float(ST), bias="bth")
+    act("q320", ("aq", me, 20, 5), scale=4.0 * ST, bias=-4.0 * ST * RND)
+    act("r64b", "r64", bias="bcc")
 
+    tt("bd", "bu", "bv4", A.add)
+    tt("be", "bu", "bv", A.add)
     tt(("cb", 10, 30), "hi", "lo", A.subtract)
+    ts("bg", "bd", RND + 2.5 - me, A.is_ge, -float(N), A.mult)
     tt(("pb", 10, 30), ("cb", 5, 25), ("cb", 0, 20), A.add)
+    tt("bs", "be", "bg", A.add)
     tt("sf", ("pb", 10, 30), ("pb", 0, 20), A.add)
+    ts("bl", "bs", me + 6.0 - 2 * RND, A.add, 19.0, A.min)
     tt("xx", "aa", "sf", A.subtract)
+    tt("ge", "sf", ("ttw", 0, 64), A.is_le, "bl")
     tt(("dd", 5, 20), ("xx", 5, 20), ("xx", 0, 15), A.subtract)
-
-    def steps(dests, b1, b2, b3, lst):
-        n = LC * len(dests)
-        for x, d in enumerate(dests):
-            act((b1, LC * x, LC * x + LC), "ttl", bias=("aa", d, d + 1))
-        for r in range(1, N):
-            for x, d in enumerate(dests):
-                o, i = (b1, n * r + LC * x, n * r + LC * x + LC), 5 * r + d
-                ts(o, ("tt", LC * r, LC * r + LC), ("sf", i, i + 1), A.is_ge, ("dd", i, i + 1), A.mult)
-        tt(b2, (b1, 0, 2 * n), (b1, 2 * n, 4 * n), A.add)
-        tt(b3, (b2, 0, n), (b2, n, 2 * n), A.add)
-        ts((lst, 0, n), b3, float(COLS - 1), A.min)
+    pick("v", ("land1q", a1, b1), "xq", own)
+    tt(("h1", 20, 84), "dd", "ge", A.mult, "bl")
+    tt("h2", ("h1", 0, 40), ("h1", 40, 80), A.add)
+    tt("h3", ("h2", 0, 20), ("h2", 20, 40), A.add)
+    ts("l2u", "h3", float(COLS - 1), A.min)
 
     own2 = (ST * me, ST * me + ST)
     pk2 = (ST * me, ST * me + PK2)
-    steps(others, "h1", "h2", "h3", "l2u")
     pick("v", "slot2q", "land1q", ("l2u", 0, 3 * LC))
-    steps([me], "g1", "g2", "g3", "lou")
+    ts(("lou", 0, LC), ("h3", 3 * LC, 4 * LC), float(COLS - 1), A.min)
+    tt("xa", ("sf", me, 20, 5), ("aq", me, 20, 5), A.subtract)
     pick("v", ("land2q",) + own2, "land1q", ("lou", 0, LC))
     pick("s", "slot2s", "land1s", ("l2u", 0, 3 * LC))
-    cp(("vland", 16 * me, 16 * me + 16), ("vout", 16 * me, 16 * me + 16), "s")
-    act("s4", "sf", scale=4.0)
     pick("s", ("land2s",) + own2, "land1s", ("lou", 0, LC))
     cut2 = lambda d: (ST * others.index(d), ST * others.index(d) + PK2)
     send("p2c", "slot2q", ("land2q",) + pk2, cut2, True)
     send("p2s", "slot2s", ("land2s",) + pk2, cut2)
 
-    quant("w")
-    tt("cf", "s4", ("eb", 0, 20), A.subtract)
-    cp("vi", "vland")
+    tt("th", "e80", "q320", A.subtract)
+    tt("cc", "xa", "r64b", A.add)
+    quant("w", 0, COLS)
     for r in range(N):
-        ts(("kk", 16 * r, 16 * r + 16), ("vland", 16 * r, 16 * r + 16), ("cf", 5 * r + me, 5 * r + me + 1), A.add,
-           float(4 * PK1 * r), A.add)
-    ts("m3", "vi", 3, A.bitwise_and)
-    ts("ks", "kk", 2, A.arith_shift_right)
-    ts("m80", "m3", float(ST), A.mult)
-    tt("f1", "m80", "ks", A.add)
+        ts(("kk", 16 * r, 16 * r + 16), ("vland", 16 * r, 16 * r + 16), ("th", r, r + 1), A.is_ge, ("cc", r, r + 1), A.add)
+    tt("f1", "vland", "kk", A.add)
     tt("f2", ("f1", 0, 32), ("f1", 32, 64), A.max)
-    tt("f3", ("f2", 0, 16), ("f2", 16, 32), A.max)
-    cp("flu", "f3")
+    for a in (0, 16):
+        tt(("f3", a, a + 16), ("f2", 0, 16), ("f2", 16, 32), A.max)
+    tr("f3t", "f3")
+    tt("f4", ("f3t", 0, 16), ("f3t", 16, 32), A.max)
+    cp("flu", "f4")
 
-    H = COLS // 2
-    halves = [(0, H, 0, 8), (H, COLS, 8, 16)]
-    for a, b, i, j in halves:
-        pick("v", ("finq", a, b), "land2q", ("flu", i, j))
-    for q, (a, b, i, j) in zip("sv", halves):
-        pick(q, ("fins", a, b), "land2s", ("flu", i, j))
-    need("t", "finq", "fins", "wq", "ws")
+    for h in (0, 1):
+        pick("v", "finq%d" % h, "land2q", ("flu", 8 * h, 8 * h + 8))
+    for h, q in enumerate("sv"):
+        pick(q, "fins%d" % h, "land2s", ("flu", 8 * h, 8 * h + 8))
     for o in range(O):
-        for h, (a, b, i, j) in enumerate(halves):
+        for h in (0, 1):
+            need("t", "finq%d" % h, "fins%d" % h, "wq", "ws")
             p, wc = 512 * (2 * o + h), (128 * o, 128 * o + 128)
-            done("t", te.matmul_mx(T.ps[:, p:p + H], ap(("wq",) + wc), ap(("ws",) + wc), ap(("finq", a, b)), ap(("fins", a, b)),
+            done("t", te.matmul_mx(T.ps[:, p:p + H], ap(("wq",) + wc), ap(("ws",) + wc), ap("finq%d" % h), ap("fins%d" % h),
                                    True, True), ["ps%d" % p])
     for o in range(O):
-        for h, q in enumerate("vs"):
+        for h, q in enumerate("sv"):
             p, y = 512 * (2 * o + h), ("yb%d" % o, H * h, H * h + H)
             need(q, "ps%d" % p)
             done(q, v.tensor_copy(ap(y), T.ps[:, p:p + H]) if q == "v" else s.activation(ap(y), T.ps[:, p:p + H], F.Copy), [y])

from concourse.bass import DstId, RemoteDMATransfer
from concourse.mybir import dt, AluOpType, ActivationFunctionType

N, COLS, O = 4, 256, 2
H = COLS // 2
PK1 = COLS // N
PK2 = COLS // N + N - 1
ST = 80
LC = ST // 16
W1 = N * ST
W2 = N * COLS
NONE = -8192.0
RND = 160.0
MID = 128.0
BUFFERS = {
    "float8_e4m3fn_x4": "xq 256 wq 256 slot1q 192 land1q 256 slot2q 240 land2q 320 finq0 128 finq1 128",
    "uint8": "xs 256 ws 256 slot1s 192 land1s 256 slot2s 240 land2s 320 fins0 128 fins1 128",
    "bfloat16": "xb 1024 wb 1024 zb 64 restart 64 low0 64 val1 256 ec 32 ind 64 indt 64 cr 64 crt 64 cum 64 z 64 pp 64 pm 64 pm2 32 "
                "bc 64 bt 64 win1 320 wt1 320 vt 16 prow 128 win2 1024 vo 64 vland 64 cn 4 cland 32 aa 20 aq 20 bu 4 bv 4",
    "float32": "odd 1 odd5 1 odd8 1 bth 1 bcc 1 start 1 q0 1 q1 1 lowf 1 selm 1 sela 1 selb 1 tti 5 ttl 5 twi 80 ttw 80 cji 4 cj 4 "
               "bv4 4 bd 4 bg 4 be 4 bs 4 r64 4 r64b 4 pos 16 t1 16 t2 16 eb 21 lo 20 hi 20 sf 20 xx 20 dd 20 ge 64 h1 84 h2 40 h3 20 "
               "e80 4 q320 4 th 4 xa 4 cc 4 kk 64 f1 64 f2 32 f3 32 f3t 32 f4 16 yb0 256 yb1 256",
    "int32": "part 1 par 1 low 1 mq 1 gm 1 la 1 lb 1 bit 1 ew 16 si 16 cb 30 pb 30 selk 4",
    "uint16": "off1 16 l1u 16 eu 16 l2u 20 lou 6 flu 16 sel 2 selh 2 selz 4 bl 4",
}
SCRATCH = {"ps": ("psum", [128, 2048], "float32")}
for _t, _l in BUFFERS.items():
    _w = _l.split()
    for _n, _c in zip(_w[0::2], _w[1::2]):
        SCRATCH[_n] = ("sbuf", [128, int(_c)], _t)
SEMAPHORES = "sv sa sg st ld_e ld_x ld_w vf vr vo vw cnt p1c p1s plc p2c p2s sent yo".split()


def plan(src, cores, topo):
    near = set(topo.cores_of(src))
    far = [d for d in cores if d not in near]
    close = [d for d in cores if d in near and d != src]
    out, used = {}, set()
    for group in (far, close):
        if group:
            eng = [e for e in topo.engines(src, group[0]) if e not in used]
            per = len(eng) // len(group)
            for i, d in enumerate(group):
                out[d] = eng[per * i:per * (i + 1)]
            used.update(eng)
    return out


def rank_program(g, core, T, topo):
    me = T.rank_of(core)
    if me is None:
        return
    A, F = AluOpType, ActivationFunctionType
    S = T.sem
    turn = [(me + 1 + i) % N for i in range(N)]
    others = turn[:N - 1]
    mine = plan(core, T.cores, topo)
    arrive = sum(len(plan(T.cores[r], T.cores, topo)[core]) for r in others)
    leave = sum(len(e) for e in mine.values())
    v, s, te, sy = g.vector, g.scalar, g.tensor, g.sync
    own_sem = {"v": "sv", "s": "sa", "g": "sg", "t": "st"}
    queue = {"v": v, "s": s, "g": g, "t": te, "y": sy}
    cnt = {k: 0 for k in SEMAPHORES}
    made = {}
    seen = {}

    def hold(q, sem, k):
        if seen.get((q, sem), 0) < k:
            queue[q].wait_ge(S[sem], k)
            seen[q, sem] = k

    def need(q, *names):
        for n in names:
            for sem, k in made.get(n, {}).items():
                hold(q, sem, k)

    def ap(x):
        return T[x][:] if not isinstance(x, tuple) else T[x[0]][:, slice(*x[1:])]

    def name(x):
        return x[0] if isinstance(x, tuple) else x

    def named(*xs):
        return [name(x) for x in xs if isinstance(x, (str, tuple))]

    def val(x):
        return ap(x) if isinstance(x, (str, tuple)) else x

    def done(q, ins, out, sem=None, by=1):
        sem = sem or own_sem[q]
        ins.then_inc(S[sem], by)
        cnt[sem] += by
        for o in out:
            made.setdefault(name(o), {})[sem] = cnt[sem]

    def cp(out, i, q="v"):
        need(q, name(i))
        done(q, v.tensor_copy(ap(out), ap(i)) if q == "v" else s.activation(ap(out), ap(i), F.Copy), [out])

    def tt(out, a, b, op, offs=None):
        need("v", *named(a, b, offs))
        a = ap(a) if offs is None else ap(a).indirect(ap(offs))
        done("v", v.tensor_tensor(ap(out), a, ap(b), op), [out])

    def ts(out, a, s1, op, s2=None, op2=None):
        need("v", *named(a, s1, s2))
        a, s1, s2 = ap(a), val(s1), val(s2)
        done("v", v.tensor_scalar(ap(out), a, s1, s2, op, op2) if op2 else v.tensor_scalar(ap(out), a, s1, None, op), [out])

    def tr(out, i):
        need("v", i)
        done("v", v.transpose(ap(out), ap(i)), [out])

    def scan(out, a, b, initial, op0, op1):
        need("v", *named(a, b, initial))
        done("v", v.tensor_tensor_scan(ap(out), ap(a), ap(b), val(initial), op0, op1), [out])

    def fill(x, c):
        done("v", v.memset(ap(x), c), [x])

    def iota(out, pat, base=0, cm=0, whole=False):
        kw = {} if whole else {"allow_small_or_imprecise_dtypes": True}
        done("g", g.iota(ap(out), pat, base, cm, **kw), [out])

    def act(out, i, **kw):
        need("s", *named(i, *kw.values()))
        done("s", s.activation(ap(out), ap(i), F.Identity, **{k: val(x) for k, x in kw.items()}), [out])

    def load(q, out, src, sem):
        done(q, queue[q].dma_start(ap(out), src), [out], sem, 16)

    def quant(k, a, b):
        need("v", k + "b")
        done("v", v.quantize_mx(ap((k + "q", a, b)), ap((k + "s", a, b)), ap((k + "b", 4 * a, 4 * b))), [k + "q", k + "s"])

    def pick(q, out, win, offs):
        need(q, win, name(offs))
        if win[-1] == "q":
            done(q, v.tensor_copy(ap(out).bitcast(dt.uint32), ap(win).bitcast(dt.uint32).indirect(ap(offs))), [out])
        elif q == "v":
            done(q, v.tensor_copy(ap(out), ap(win).indirect(ap(offs))), [out])
        else:
            done(q, s.activation(ap(out), ap(win).indirect(ap(offs)), F.Copy), [out])

    def send(sem, buf, dst, cut, codes=False):
        need("g", buf)
        raw = (lambda t: t.bitcast(dt.uint8)) if codes else (lambda t: t)
        tl = []
        for d in others:
            rid, pid = topo.addr(T.cores[d], core)
            tl.append(RemoteDMATransfer(dst_ids=[DstId(rid=rid, pnc=pid)], dma_engine_mask=sum(1 << e for e in mine[T.cores[d]]),
                                        remote_sem=S[sem], src=raw(ap((buf,) + cut(d))), dst=raw(ap(dst))))
        g.remote_dma_fused(tl, local_sem=S.sent)
        cnt["sent"] += leave
        made.setdefault(name(dst), {})[sem] = arrive

    for q, k0 in (("y", 0), ("s", 4)):
        for k in range(k0, k0 + 4):
            done(q, queue[q].dma_start(T.ew[16 * k:16 * k + 16, :], T.to[:, :]), ["ew"], "ld_e", 16)
    load("y", "xb", T.x[:, :], "ld_x")
    load("y", "wb", T.w[:, :], "ld_w")
    fill("zb", 0.0)
    fill(("win2", 0, COLS), NONE)
    need("y", "win2")
    for a in range(COLS, W2, COLS):
        done("y", sy.dma_start(T.win2[:, a:a + COLS], T.win2[:, 0:COLS]), ["blank"], "vf", 16)

    iota("part", [[1, 1]], 0, 1, True)
    iota("selk", [[16, 4]], 15, 0, True)
    iota("val1", [[1, 16], [16, 16]])
    iota("cji", [[16, 4]])
    iota("twi", [[-PK1, 4], [0, N], [16, LC]], -PK1)
    iota("tti", [[16, LC]], -int(RND))
    iota(("cb", 0, 10), [[0, 10]], 0, 0, True)
    iota(("pb", 0, 10), [[0, 10]], 0, 0, True)
    iota("r64", [[PK1, N]], int(RND + MID) - 1)
    ts("par", "part", 4, A.logical_shift_right, 1, A.bitwise_and)
    ts("low", "part", 15, A.bitwise_and)
    ts("mq", "part", 2, A.logical_shift_right, 3, A.bitwise_and)
    cp("odd", "par")
    cp("lowf", "low")
    tt("la", "low", "mq", A.add)
    ts("gm", "low", 4 * (N - 1 - me) - 0.5, A.is_ge, -float(N * LC), A.mult)
    ts("q0", "odd", 3.0, A.mult, RND, A.add)
    ts("q1", "odd", RND + 1.0, A.add)
    tt("lb", "la", "gm", A.add)
    ts("bit", "lb", 1, A.bitwise_and)
    flip = LC * (me + 1) % 2
    act("sela", "odd", scale=16.0 - 64.0 * flip, bias=16.0 * LC * (me + 1) + 32.0 * flip)
    act("selm", "odd", scale=-64.0 * (1 - 2 * flip), bias=32.0 * (1 - 2 * flip))
    act("odd8", "odd", scale=8.0)
    act("start", "odd", scale=-(COLS - 1.0))
    act("restart", ("zb", 0, 64), bias=1.0)
    act("low0", ("zb", 0, 64), bias=-NONE)
    act("odd5", "odd", scale=1.0 / LC)
    need("s", "restart", "low0")
    act(("restart", 0, 64, 16), ("zb", 0, 4))
    act(("low0", 16, 17), ("zb", 0, 1), bias=("start", 0, 1))
    act("eb", ("zb", 0, 21))
    act(("dd", 0, 5), ("zb", 0, 5))
    act(("cn", 3, 4), ("zb", 0, 1), bias=float(COLS))
    need("s", "eb")
    act(("eb", 4, 20, 5), ("zb", 0, 4), bias=float(COLS))
    act(("win1", 0, COLS), "val1", scale=0.0)
    act(("win1", COLS, W1), ("zb", 0, W1 - COLS))
    act("prow", ("val1", 0, H), scale=0.0)
    ts("selb", "bit", ("selm", 0, 1), A.mult, ("sela", 0, 1), A.add)
    cp("selz", "selk")
    ts(("sel", 0, 1), "lb", 16.0, A.mult, ("selb", 0, 1), A.add)
    ts(("selh", 0, 1), "low", ("odd8", 0, 1), A.add, 15.0, A.min)

    for a in (0, 16):
        ts(("ec", a, a + 16), "ew", 1.0 / COLS, A.mult, RND - 0.498, A.add)
    for u in (0, 1):
        ts(("ind", 32 * u, 32 * u + 32), "ec", ("q%d" % u, 0, 1), A.is_equal)
    tr("indt", "ind")
    scan("cr", "restart", "indt", 0.0, A.mult, A.add)
    tr("crt", "cr")
    scan(("cum", 0, 48), ("low0", 0, 48), ("crt", 0, 48), ("start", 0, 1), A.min, A.add)
    scan(("cum", 48, 64), ("low0", 48, 64), ("crt", 48, 64), ("cum", 31, 32), A.min, A.add)
    tr("z", "cum")
    tt("pp", "z", "cr", A.subtract, "selz")
    for i, c in enumerate((31, 47)):
        act(("bc", 32 * i, 32 * i + 32), ("zb", 0, 32), bias=("cum", c, c + 1))
    tt("pm", "pp", "indt", A.mult)
    tr("bt", "bc")
    tt("pm2", ("pm", 0, 32), ("pm", 32, 64), A.add)
    tt("pos", ("pm2", 0, 16), ("pm2", 16, 32), A.subtract)
    ts("si", "pos", 0.25, A.mult, -0.375, A.add)
    ts("t1", "si", -(4.0 * ST - 1) / ST, A.mult, ("odd5", 0, 1), A.add)
    tt("t2", "pos", "t1", A.add)
    ts("off1", "t2", float(ST), A.mult)

    act(("cn", 0, 3), ("bt", 15, 48, 16))
    cp(("cland", 8 * me, 8 * me + 4), "cn", "s")
    act("vt", "t2", scale=float(ST), bias=-MID)
    for q, a, r in (("y", 0, 0), ("s", 24, 16)):
        need(q, "vt", "prow")
        for p in range(0, 128, 32):
            done(q, queue[q].dma_start(T.prow[p + r:p + r + 1, :], T.vt[p + a:p + a + 8, :]), ["rows"], "vr", 16)
    act("cj", "cji", bias="lowf")
    act("ttl", "tti", bias="lowf")
    act("ttw", "twi", bias="lowf")
    act("bu", "cj", scale=0.2, bias=RND - 0.4)
    act("bv", "cj", scale=0.05, bias=RND - 0.475)
    act("bth", "odd", scale=16.0, bias=-MID - 0.5)
    act("bcc", "odd", scale=-16.0)
    act("bv4", "bv", scale=-4.0, bias=4 * RND)

    need("v", "val1", "off1", "win1")
    done("v", v.tensor_copy(T.win1[:, 0:W1].indirect(T.off1[:, 0:16]), T.val1[:, 0:COLS]), ["win1"])
    quant("x", 0, H)
    tr("wt1", "win1")
    quant("x", H, COLS)
    need("v", "wt1", "sel")
    done("v", v.tensor_copy(T.l1u[:], T.wt1[:, 0:W1].indirect(T.sel[:, 0:1])), ["l1u"])
    a1, b1 = PK1 * me, PK1 * (me + 1)
    mix, own = ("l1u", 0, 12), ("l1u", 12, 16)
    pick("v", "slot1q", "xq", mix)
    pick("s", "slot1s", "xs", mix)
    pick("s", ("land1s", a1, b1), "xs", own)

    send("cnt", "cn", ("cland", 8 * me, 8 * me + 4), lambda d: (0, 4))
    cut1 = lambda d: (PK1 * others.index(d), PK1 * (others.index(d) + 1))
    send("p1c", "slot1q", ("land1q", a1, b1), cut1, True)
    send("p1s", "slot1s", ("land1s", a1, b1), cut1)

    need("v", "ew", "selh")
    done("v", v.tensor_copy(T.eu[:], T.ew[:, 0:16].indirect(T.selh[:, 0:1])), ["eu"])
    need("v", "rows", "prow", "eu", "win2", "blank")
    done("v", v.tensor_copy(T.win2[:, 0:W2].indirect(T.eu[:, 0:8]), T.prow[:, 0:H]), ["win2"])
    need("y", "win2")
    for d in turn:
        out = ("vo", 16 * d, 16 * d + 16) if d != me else ("vland", 16 * d, 16 * d + 16)
        done("y", sy.dma_start(ap(out), T.win2[0:128:16, COLS * d:COLS * d + COLS]), [out], "vo" if d != me else "vw", 16)
    send("plc", "vo", ("vland", 16 * me, 16 * me + 16), lambda d: (16 * d, 16 * d + 16))

    for i, q, kw in ((0, 1, {}), (2, 2, {}), (1, 3, {"scale": -1.0, "bias": 1.0})):
        act(("eb", q, 20, 5), ("cland", i, 32, 8), **kw)
    act("lo", ("eb", 0, 20), scale=0.25)
    act("hi", ("eb", 1, 21), scale=0.25, bias=0.375 - PK1)
    act("aa", ("eb", 0, 20), scale=0.25, bias=RND + (N - 1 - me) / 4.0 - 0.375)
    for x, d in enumerate(turn):
        act(("h1", LC * x, LC * x + LC), "ttl", bias=("aa", d, d + 1))
    act("aq", ("eb", 0, 20), scale=0.25, bias=RND - 0.375)
    act("e80", ("eb", me, 20, 5), scale=float(ST), bias="bth")
    act("q320", ("aq", me, 20, 5), scale=4.0 * ST, bias=-4.0 * ST * RND)
    act("r64b", "r64", bias="bcc")

    tt("bd", "bu", "bv4", A.add)
    tt("be", "bu", "bv", A.add)
    tt(("cb", 10, 30), "hi", "lo", A.subtract)
    ts("bg", "bd", RND + 2.5 - me, A.is_ge, -float(N), A.mult)
    tt(("pb", 10, 30), ("cb", 5, 25), ("cb", 0, 20), A.add)
    tt("bs", "be", "bg", A.add)
    tt("sf", ("pb", 10, 30), ("pb", 0, 20), A.add)
    ts("bl", "bs", me + 6.0 - 2 * RND, A.add, 19.0, A.min)
    tt("xx", "aa", "sf", A.subtract)
    tt("ge", "sf", ("ttw", 0, 64), A.is_le, "bl")
    tt(("dd", 5, 20), ("xx", 5, 20), ("xx", 0, 15), A.subtract)
    pick("v", ("land1q", a1, b1), "xq", own)
    tt(("h1", 20, 84), "dd", "ge", A.mult, "bl")
    tt("h2", ("h1", 0, 40), ("h1", 40, 80), A.add)
    tt("h3", ("h2", 0, 20), ("h2", 20, 40), A.add)
    ts("l2u", "h3", float(COLS - 1), A.min)

    own2 = (ST * me, ST * me + ST)
    pk2 = (ST * me, ST * me + PK2)
    pick("v", "slot2q", "land1q", ("l2u", 0, 3 * LC))
    ts(("lou", 0, LC), ("h3", 3 * LC, 4 * LC), float(COLS - 1), A.min)
    tt("xa", ("sf", me, 20, 5), ("aq", me, 20, 5), A.subtract)
    pick("v", ("land2q",) + own2, "land1q", ("lou", 0, LC))
    pick("s", "slot2s", "land1s", ("l2u", 0, 3 * LC))
    pick("s", ("land2s",) + own2, "land1s", ("lou", 0, LC))
    cut2 = lambda d: (ST * others.index(d), ST * others.index(d) + PK2)
    send("p2c", "slot2q", ("land2q",) + pk2, cut2, True)
    send("p2s", "slot2s", ("land2s",) + pk2, cut2)

    tt("th", "e80", "q320", A.subtract)
    tt("cc", "xa", "r64b", A.add)
    quant("w", 0, COLS)
    for r in range(N):
        ts(("kk", 16 * r, 16 * r + 16), ("vland", 16 * r, 16 * r + 16), ("th", r, r + 1), A.is_ge, ("cc", r, r + 1), A.add)
    tt("f1", "vland", "kk", A.add)
    tt("f2", ("f1", 0, 32), ("f1", 32, 64), A.max)
    for a in (0, 16):
        tt(("f3", a, a + 16), ("f2", 0, 16), ("f2", 16, 32), A.max)
    tr("f3t", "f3")
    tt("f4", ("f3t", 0, 16), ("f3t", 16, 32), A.max)
    cp("flu", "f4")

    for h in (0, 1):
        pick("v", "finq%d" % h, "land2q", ("flu", 8 * h, 8 * h + 8))
    for h, q in enumerate("sv"):
        pick(q, "fins%d" % h, "land2s", ("flu", 8 * h, 8 * h + 8))
    for o in range(O):
        for h in (0, 1):
            need("t", "finq%d" % h, "fins%d" % h, "wq", "ws")
            p, wc = 512 * (2 * o + h), (128 * o, 128 * o + 128)
            done("t", te.matmul_mx(T.ps[:, p:p + H], ap(("wq",) + wc), ap(("ws",) + wc), ap("finq%d" % h), ap("fins%d" % h),
                                   True, True), ["ps%d" % p])
    for o in range(O):
        for h, q in enumerate("sv"):
            p, y = 512 * (2 * o + h), ("yb%d" % o, H * h, H * h + H)
            need(q, "ps%d" % p)
            done(q, v.tensor_copy(ap(y), T.ps[:, p:p + H]) if q == "v" else s.activation(ap(y), T.ps[:, p:p + H], F.Copy), [y])
    for o, q in enumerate("ys"):
        need(q, "yb%d" % o)
        done(q, queue[q].dma_start(T.y[:, COLS * o:COLS * o + COLS], T["yb%d" % o][:]), ["out"], "yo", 16)
    hold("y", "yo", cnt["yo"])
    hold("g", "sent", cnt["sent"])
    hold("g", "sg", cnt["sg"])
